import numpy as np
import ml_dtypes


def mxq(x, axis, fmt="e4m3"):
    dtype, down = {"e4m3": (ml_dtypes.float8_e4m3fn, 7), "e5m2": (ml_dtypes.float8_e5m2, 14)}[fmt]
    v = np.moveaxis(np.asarray(x, np.float32).astype(ml_dtypes.bfloat16).astype(np.float64), axis, -1)
    blocks = v.reshape(v.shape[:-1] + (-1, 32))
    amax = np.abs(blocks).max(-1, keepdims=True)
    byte = np.maximum(np.where(amax > 0, np.frexp(amax)[1] - 1 + 127, 0) - down, 1)
    scale = np.exp2(byte - 127.0)
    codes = (blocks / scale).astype(np.float32).astype(dtype).astype(np.float64)
    return np.moveaxis((codes * scale).reshape(v.shape), -1, axis)


WIDE = False


def mx_kscale(k):
    if not WIDE:
        return np.ones(k)
    levels = np.array([10, -10, 5, -5, 0])
    if k % 512:
        return np.exp2(np.random.permutation(np.resize(levels, k // 32))).repeat(32)
    a = np.empty((k // 512, 16))
    for p in range(k // 512):
        a[p, :8] = np.random.permutation(np.resize(levels, 8))
        for g in range(8):
            far = levels[np.abs(levels - a[p, g]) >= 10]
            a[p, g + 8] = far[np.random.randint(len(far))]
    return np.exp2(a.ravel()).repeat(32)


def f64(x):
    return np.asarray(x).astype(np.float64)


def striped(idx):
    return np.tile(idx.reshape(-1, 16).T, (8, 1)).astype(np.uint16)


def unstriped(offs):
    return offs[:16].T.reshape(-1).astype(np.int64)


E2M1 = np.array([0.0, 0.5, 1.0, 1.5, 2.0, 3.0, 4.0, 6.0, -0.0, -0.5, -1.0, -1.5, -2.0, -3.0, -4.0, -6.0])


def pack_weight(w, fmt):
    k, n = w.shape
    w = f64(np.asarray(w, np.float32).astype(ml_dtypes.bfloat16)).reshape(k // 32, 32, n)
    amax = np.abs(w).max(1)
    if fmt == "e4m3":
        byte = np.frexp(amax)[1] - 1 + 127 - 7
    else:
        mant, ex = np.frexp(amax / 6.0)
        byte = np.where(mant > 0.5, ex, ex - 1) + 127
    byte = np.clip(np.where(amax > 0, byte, 1), 1, 254)
    scaled = (w * np.exp2(127.0 - byte)[:, None, :]).reshape(k, n).astype(np.float32)
    by_word = np.ascontiguousarray(scaled.reshape(k // 512, 128, 4, n).transpose(0, 1, 3, 2))
    if fmt == "e4m3":
        words = by_word.astype(ml_dtypes.float8_e4m3fn).view(np.uint8)
    else:
        c = by_word.astype(ml_dtypes.float4_e2m1fn).view(np.uint8) & 0xF
        words = (c[..., 0::2] | (c[..., 1::2] << 4)).reshape(k // 512, 128, 2 * n)
    return np.ascontiguousarray(words), np.ascontiguousarray(byte.astype(np.uint8).reshape(k // 512, 16, n))


def unpack_weight(words, scales, fmt):
    g, _, n = scales.shape
    words = np.ascontiguousarray(words).reshape(g, 128, n, -1)
    if fmt == "e4m3":
        vals = words.view(ml_dtypes.float8_e4m3fn).astype(np.float64)
    else:
        nib = np.empty((g, 128, n, 4), np.uint8)
        nib[..., 0::2] = words & 0xF
        nib[..., 1::2] = words >> 4
        vals = E2M1[nib]
    vals = vals * np.repeat(np.exp2(scales.astype(np.float64) - 127.0), 8, axis=1)[..., None]
    return vals.transpose(0, 1, 3, 2).reshape(g * 512, n)


def gelu(v):
    return 0.5 * v * (1.0 + np.tanh(np.sqrt(2.0 / np.pi) * (v + 0.044715 * v**3)))


K, H, N, T, S, P, T2 = 1024, 512, 768, 4096, 1024, 1024, 2048

def setup_inputs():
    n = np.random.standard_normal
    s = mx_kscale(K)[:, None]
    u = mx_kscale(H)[:, None]
    d = {}
    d["tab_words"], d["tab_scales"] = pack_weight(n((K, T)) * s, "e4m3")
    d["offs"] = striped(np.random.permutation(T)[:S])
    d["offs2"] = striped(np.random.permutation(T2)[:S])
    d["offs3"] = striped(np.random.permutation(T2)[:P])
    d["offs4"] = striped(np.random.permutation(T2)[:P])
    d["w1"] = (1.5 * n((K, H)) / K ** 0.5 / s).astype(np.float32)
    d["w2_words"], d["w2_scales"] = pack_weight(n((K, H)) / K ** 0.5 / s, "e4m3")
    d["cyc"] = n((H, S)).astype(np.float32)
    d["gain"] = (np.exp(0.3 * n(H)) * u[:, 0]).astype(np.float32)
    d["wgs"] = np.exp(0.3 * n((128, S))).astype(np.float32)
    d["page0"] = (n((H, T2)) * u).astype(np.float32)
    d["lo"] = (0.4 * n(H) * u[:, 0]).astype(np.float32)
    d["w3"] = (1.4 * n((H, N)) / H ** 0.5 / u).astype(np.float32)
    d["w4_words"], d["w4_scales"] = pack_weight(n((H, N)) / H ** 0.5 / u, "e2m1")
    d["wgo"] = np.exp(0.3 * n((128, P))).astype(np.float32)
    d["page1"] = n((N, T2)).astype(np.float32)
    return d

def reference(tab_words, tab_scales, offs, offs2, offs3, offs4, w1, w2_words, w2_scales, cyc, gain, wgs, page0, lo, w3, w4_words, w4_scales, wgo, page1):
    v = unpack_weight(tab_words, tab_scales, "e4m3")[:, unstriped(offs)]
    a = mxq(f64(w1), 0, "e4m3").T @ v
    b = unpack_weight(w2_words, w2_scales, "e4m3").T @ v
    h = (np.tanh(a) * f64(cyc) + b) * f64(gain)[:, None]
    page = f64(page0).copy()
    page[:, unstriped(offs2)] = np.tile(f64(wgs), (H // 128, 1)) * h
    x = np.maximum(page[:, unstriped(offs3)], f64(lo)[:, None])
    xq = mxq(x, 0, "e4m3")
    hq = mxq(h, 0, "e4m3")
    y1 = mxq(f64(w3), 0, "e4m3").T @ xq
    y2 = unpack_weight(w4_words, w4_scales, "e2m1").T @ hq
    y = np.maximum(y1, y2)
    out = f64(page1).copy()
    out[:, unstriped(offs4)] = np.tile(f64(wgo), (N // 128, 1)) * y
    return out

@@ -1,0 +1,325 @@
+from contextlib import ExitStack
+
+import concourse.mybir as mybir
+from concourse.masks import make_identity
+
+K, H, N, T, S, T2 = 1024, 512, 768, 4096, 1024, 2048
+FLOPS = 2 * S * (2 * K * H + 2 * H * N)
+
+F32 = mybir.dt.float32
+BF16 = mybir.dt.bfloat16
+I32 = mybir.dt.int32
+U32 = mybir.dt.uint32
+U16 = mybir.dt.uint16
+U8 = mybir.dt.uint8
+FP8X4 = mybir.dt.float8_e4m3fn_x4
+FP4X4 = mybir.dt.float4_e2m1fn_x4
+MULT = mybir.AluOpType.mult
+ADD = mybir.AluOpType.add
+MAX = mybir.AluOpType.max
+TANH = mybir.ActivationFunctionType.Tanh
+
+P = 128
+PASSES = K // 512
+SLICES = H // P
+BLOCKS = N // P
+HALF = 512
+HALVES = S // HALF
+LIST_COLS = HALF // 16
+W3_PART = N // (SLICES - 1)
+
+
+def tile_list_linen_wear_pages_kernel(
+    tc, tab_words, tab_scales, offs, offs2, offs3, offs4, w1, w2_words, w2_scales, cyc, gain, wgs,
+    page0, lo, w3, w4_words, w4_scales, wgo, page1, out,
+):
+    nc = tc.nc
+    with ExitStack() as ctx:
+        lists = ctx.enter_context(tc.tile_pool(name="lists", bufs=1))
+        keep = ctx.enter_context(tc.tile_pool(name="keep", bufs=1))
+        shared = ctx.enter_context(tc.tile_pool(name="shared", bufs=1))
+        ring = ctx.enter_context(tc.tile_pool(name="ring", bufs=2))
+        psum = ctx.enter_context(tc.psum_pool(name="psum", bufs=2))
+
+        def half_cols(h):
+            return slice(h * HALF, (h + 1) * HALF)
+
+        def half_list(tile, h):
+            return tile[:, h * LIST_COLS : (h + 1) * LIST_COLS]
+
+        def load_list(src, name):
+            tile = lists.tile([P, S // 16], U16, name=name)
+            nc.sync.dma_start(tile[:], src)
+            return tile
+
+        def scale_tile(width, name, clear):
+            tile = keep.tile([P, width], U8, name=name, align_bytes=64)
+            clear.memset(tile[:].bitcast(I32), 0)
+            return tile
+
+        def load_scale_rows(tile, src, queue):
+            passes = src.shape[0]
+            for q in range(4):
+                queue.dma_start(
+                    tile[32 * q : 32 * q + 4 * passes, :].bitcast(I32),
+                    src[:, 4 * q : 4 * q + 4, :].bitcast(I32),
+                )
+
+        def load_table_words(a):
+            tile = shared.tile([P, T], I32, name="tab_words%d" % a, offset=a * T * 4)
+            nc.sync.dma_start(tile[:], tab_words[a].rearrange("p n t -> p (n t)").bitcast(I32))
+            return tile
+
+        def load_weights(c):
+            cols = slice(c * P, (c + 1) * P)
+            raw = []
+            for a in range(PASSES):
+                tile = ring.tile([P, 4, P], F32, name="w1_raw%d" % a)
+                nc.sync.dma_start(
+                    tile[:], w1[512 * a : 512 * (a + 1), cols].rearrange("(p j) r -> p j r", j=4)
+                )
+                raw.append(tile)
+            w2c = keep.tile([P, PASSES, P], I32, name="w2_codes%d" % c, align_bytes=64)
+            nc.sync.dma_start(
+                w2c[:],
+                w2_words[:, :, cols, :].rearrange("a p n t -> p a (n t)").bitcast(I32),
+            )
+            return raw, w2c
+
+        def load_rows(src, c, name):
+            tile = keep.tile([P, src.shape[1]], F32, name="%s%d" % (name, c))
+            nc.sync.dma_start(tile[:], src[c * P : (c + 1) * P, :])
+            return tile
+
+        def interleave(dst, src):
+            nc.scalar.copy(
+                dst.rearrange("p (c i t) -> p c t i", i=4, t=4),
+                src.rearrange("p t (c i) -> p c t i", i=4),
+            )
+
+        idx = load_list(offs, "idx")
+        landed = shared.tile([P, T], U8, name="landed", offset=PASSES * T * 4)
+        load_scale_rows(landed, tab_scales, nc.sync)
+        tab_s = scale_tile(T, "tab_s", nc.vector)
+        for q in range(4):
+            rows = slice(32 * q, 32 * q + 4 * PASSES)
+            nc.vector.tensor_copy(tab_s[rows, :].bitcast(I32), landed[rows, :].bitcast(I32))
+        w2_s = scale_tile(H, "w2_s", nc.gpsimd)
+        vectors = keep.tile([P, P], F32, name="vectors")
+        nc.gpsimd.memset(vectors[:], 0.0)
+        nc.gpsimd.dma_start(vectors[0:SLICES, :], gain.rearrange("(c p) -> c p", p=P))
+        nc.gpsimd.dma_start(vectors[SLICES : 2 * SLICES, :], lo.rearrange("(c p) -> c p", p=P))
+        ident = keep.tile([P, P], F32, name="ident")
+        make_identity(nc, ident[:])
+        w4_s = scale_tile(N, "w4_s", nc.gpsimd)
+        turned_vectors = psum.tile([P, P], F32, name="turn_a")
+        nc.tensor.transpose(turned_vectors[:], vectors[:], ident[:])
+        per_row = keep.tile([P, 2 * SLICES], F32, name="per_row")
+        nc.scalar.copy(per_row[:], turned_vectors[:, 0 : 2 * SLICES])
+        gain_c = per_row[:, 0:SLICES]
+        lo_c = per_row[:, SLICES : 2 * SLICES]
+
+        words = [load_table_words(0)]
+        weights = [load_weights(0)]
+        load_scale_rows(w2_s, w2_scales, nc.sync)
+        words.append(load_table_words(1))
+        cycs = [load_rows(cyc, 0, "cyc")]
+        wgs_sb = load_rows(wgs, 0, "wgs")
+        idx2 = load_list(offs2, "idx2")
+        pages0 = []
+
+        v_codes = [[None] * HALVES for a in range(PASSES)]
+        v_scales = keep.tile([P, S], U8, name="v_scales", align_bytes=64)
+        nc.vector.tensor_copy(v_scales[:], tab_s[:].indirect(idx[:]))
+        for a in range(PASSES):
+            for h in range(HALVES):
+                picked = keep.tile([P, HALF], U32, name="v_codes%d%d" % (a, h), align_bytes=64)
+                nc.vector.tensor_copy(picked[:], words[a][:].bitcast(U32).indirect(half_list(idx, h)))
+                v_codes[a][h] = picked
+
+        def quantise_w1(c):
+            raw = weights[c][0]
+            grouped = ring.tile([P, PASSES * 4 * P], BF16, name="w1_grouped", align_bytes=64)
+            for a in range(PASSES):
+                interleave(grouped[:, a * 4 * P : (a + 1) * 4 * P], raw[a][:])
+            codes = ring.tile([P, PASSES * P], U32, name="w1_codes", align_bytes=64)
+            scales = ring.tile([P, PASSES * P], U8, name="w1_scales", align_bytes=64)
+            nc.vector.quantize_mx(codes[:].bitcast(FP8X4), scales[:], grouped[:])
+            return codes, scales
+
+        def turn_rows(values, turned, c):
+            bank = psum.tile([P, 4, P], F32, name="turn_a")
+            for b in range(4):
+                nc.tensor.transpose(bank[:, b, :], values[:, b * P : (b + 1) * P], ident[:])
+            nc.scalar.copy(
+                turned[:].rearrange("j b (u p e) -> j b u p e", u=2, e=2)[:, :, :, 32 * c : 32 * (c + 1), :],
+                bank[:].rearrange("j b (q u e) -> j b u q e", u=2, e=2),
+            )
+
+        def turn_back(turned):
+            pairs = turned[:].rearrange("j b w -> j (b w)").bitcast(F32)
+            grouped = ring.tile([P, 4 * HALF], BF16, name="grouped", align_bytes=64)
+            for g in range(2):
+                bank = psum.tile([P, 2, 2, P], F32, name="turn_b")
+                for b in range(2):
+                    for u in range(2):
+                        first = (2 * (2 * g + b) + u) * P
+                        nc.tensor.transpose(bank[:, b, u, :], pairs[:, first : first + P], ident[:])
+                nc.scalar.copy(
+                    grouped[:].bitcast(F32)[:, g * 4 * P : (g + 1) * 4 * P].rearrange(
+                        "p (b j u) -> p b j u", b=2, u=2
+                    ),
+                    bank[:].rearrange("p b u j -> p b j u"),
+                )
+            return grouped
+
+        def quantise_half(grouped, name):
+            codes = keep.tile([P, HALF], U32, name=name + "_codes", align_bytes=64)
+            scales = keep.tile([P, HALF], U8, name=name + "_scales", align_bytes=64)
+            nc.vector.quantize_mx(codes[:].bitcast(FP8X4), scales[:], grouped[:])
+            return codes, scales
+
+        w3_codes = keep.tile([P, N], U32, name="w3_codes", align_bytes=64)
+        w3_scales = keep.tile([P, N], U8, name="w3_scales", align_bytes=64)
+
+        def quantise_w3(part):
+            cols = slice(part * W3_PART, (part + 1) * W3_PART)
+            raw = ring.tile([P, 4, W3_PART], F32, name="w3_raw")
+            nc.sync.dma_start(raw[:], w3[:, cols].rearrange("(p j) n -> p j n", j=4))
+            grouped = ring.tile([P, 4 * W3_PART], BF16, name="w3_grouped", align_bytes=64)
+            interleave(grouped[:], raw[:])
+            nc.vector.quantize_mx(w3_codes[:, cols].bitcast(FP8X4), w3_scales[:, cols], grouped[:])
+
+        h_turned = [keep.tile([P, 4, H], BF16, name="h_turned%d" % h) for h in range(HALVES)]
+        w1_q = quantise_w1(0)
+        for c in range(SLICES):
+            if c + 1 < SLICES:
+                weights.append(load_weights(c + 1))
+            page_c = load_rows(page0, c, "page0_")
+            pages0.append(page_c)
+            if c + 1 < SLICES:
+                cycs.append(load_rows(cyc, c + 1, "cyc"))
+            w1_codes, w1_scales = w1_q
+            w2c = weights[c][1]
+            cyc_c = cycs[c]
+            cols = slice(c * P, (c + 1) * P)
+            h_c = ring.tile([P, S], F32, name="h_c")
+            prods = []
+            sums = []
+            for h in range(HALVES):
+                sum_a = psum.tile([P, HALF], F32, name="sum_a")
+                sum_b = psum.tile([P, HALF], F32, name="sum_b")
+                for a in range(PASSES):
+                    nc.tensor.matmul_mx(
+                        sum_a[:],
+                        lhsT=w1_codes[:, a * P : (a + 1) * P].bitcast(FP8X4),
+                        lhsT_scale=w1_scales[:, a * P : (a + 1) * P],
+                        rhs=v_codes[a][h][:].bitcast(FP8X4),
+                        rhs_scale=v_scales[4 * a :, half_cols(h)],
+                        start=(a == 0),
+                        stop=(a == PASSES - 1),
+                    )
+                for a in range(PASSES):
+                    nc.tensor.matmul_mx(
+                        sum_b[:],
+                        lhsT=w2c[:, a, :].bitcast(FP8X4),
+                        lhsT_scale=w2_s[4 * a :, cols],
+                        rhs=v_codes[a][h][:].bitcast(FP8X4),
+                        rhs_scale=v_scales[4 * a :, half_cols(h)],
+                        start=(a == 0),
+                        stop=(a == PASSES - 1),
+                    )
+                squashed = ring.tile([P, HALF], F32, name="squashed", tag="ring_a", bufs=4)
+                nc.scalar.activation(squashed[:], sum_a[:], TANH)
+                prod = ring.tile([P, HALF], F32, name="prod", tag="ring_b", bufs=4)
+                nc.vector.scalar_tensor_tensor(
+                    prod[:], squashed[:], gain_c[:, c : c + 1], cyc_c[:, half_cols(h)], MULT, MULT
+                )
+                prods.append(prod)
+                sums.append(sum_b)
+            for h in range(HALVES):
+                nc.vector.scalar_tensor_tensor(
+                    h_c[:, half_cols(h)], sums[h][:], gain_c[:, c : c + 1], prods[h][:], MULT, ADD
+                )
+            if c + 1 < SLICES:
+                w1_q = quantise_w1(c + 1)
+            if c > 0:
+                quantise_w3(c - 1)
+            nc.vector.tensor_tensor(page_c[:].indirect(idx2[:]), h_c[:], wgs_sb[:], MULT)
+            for h in range(HALVES):
+                turn_rows(h_c[:, half_cols(h)], h_turned[h], c)
+
+        w4_codes = keep.tile([P, 2 * N], U8, name="w4_codes", align_bytes=64)
+        nc.sync.dma_start(w4_codes[:].bitcast(I32), w4_words[0].bitcast(I32))
+        load_scale_rows(w4_s, w4_scales, nc.sync)
+        idx4 = load_list(offs4, "idx4")
+        wgo_sb = keep.tile([P, S], F32, name="wgo_sb")
+        nc.sync.dma_start(wgo_sb[:], wgo)
+        pages = []
+        for nb in range(BLOCKS):
+            page = shared.tile([P, T2], F32, name="page1_%d" % nb, offset=nb * T2 * 4)
+            nc.sync.dma_start(page[:], page1[nb * P : (nb + 1) * P, :])
+            pages.append(page)
+            if nb == 1:
+                idx3 = load_list(offs3, "idx3")
+
+        h_grouped = [turn_back(h_turned[h]) for h in range(HALVES)]
+
+        def recall(h):
+            turned = keep.tile([P, 4, H], BF16, name="x_turned%d" % h)
+            fetched = {}
+            for step in range(SLICES + 1):
+                if step < SLICES:
+                    c = step
+                    fetched[c] = ring.tile([P, HALF], F32, name="fetched", tag="ring_a", bufs=4)
+                    nc.vector.tensor_copy(fetched[c][:], pages0[c][:].indirect(half_list(idx3, h)))
+                if step > 0:
+                    c = step - 1
+                    floored = ring.tile([P, HALF], F32, name="floored", tag="ring_b", bufs=4)
+                    nc.vector.tensor_scalar(floored[:], fetched[c][:], lo_c[:, c : c + 1], None, MAX)
+                    turn_rows(floored[:], turned, c)
+            return turned
+
+        x_turned = recall(0)
+        h_q = [quantise_half(h_grouped[h], "h%d" % h) for h in range(HALVES)]
+        x_grouped = [turn_back(x_turned)]
+        x_grouped.append(turn_back(recall(1)))
+        x_q = [quantise_half(x_grouped[0], "x0")]
+
+        def place(nb, h):
+            cols = slice(nb * P, (nb + 1) * P)
+            sum_2 = psum.tile([P, HALF], F32, name="sum_b")
+            nc.tensor.matmul_mx(
+                sum_2[:],
+                lhsT=w4_codes[:, 2 * nb * P : 2 * (nb + 1) * P].bitcast(FP4X4),
+                lhsT_scale=w4_s[:, cols],
+                rhs=h_q[h][0][:].bitcast(FP8X4),
+                rhs_scale=h_q[h][1][:],
+                start=True,
+                stop=True,
+            )
+            y2 = ring.tile([P, HALF], F32, name="y2", tag="ring_a", bufs=4)
+            nc.scalar.copy(y2[:], sum_2[:])
+            sum_1 = psum.tile([P, HALF], F32, name="sum_a")
+            nc.tensor.matmul_mx(
+                sum_1[:],
+                lhsT=w3_codes[:, cols].bitcast(FP8X4),
+                lhsT_scale=w3_scales[:, cols],
+                rhs=x_q[h][0][:].bitcast(FP8X4),
+                rhs_scale=x_q[h][1][:],
+                start=True,
+                stop=True,
+            )
+            y = ring.tile([P, HALF], F32, name="y", tag="ring_b", bufs=4)
+            nc.vector.tensor_tensor(y[:], sum_1[:], y2[:], MAX)
+            nc.vector.tensor_tensor(
+                pages[nb][:].indirect(half_list(idx4, h)), y[:], wgo_sb[:, half_cols(h)], MULT
+            )
+
+        place(0, 0)
+        x_q.append(quantise_half(x_grouped[1], "x1"))
+        for nb in range(BLOCKS):
+            if nb + 1 < BLOCKS:
+                place(nb + 1, 0)
+            place(nb, 1)
+            nc.sync.dma_start(out[nb * P : (nb + 1) * P, :], pages[nb][:])

@@ -17,7 +17,10 @@ FP4X4 = mybir.dt.float4_e2m1fn_x4
 MULT = mybir.AluOpType.mult
 ADD = mybir.AluOpType.add
 MAX = mybir.AluOpType.max
+MIN = mybir.AluOpType.min
 TANH = mybir.ActivationFunctionType.Tanh
+COPY = mybir.ActivationFunctionType.Copy
+F32_MAX = 3.4028234663852886e38
 
 P = 128
 PASSES = K // 512
@@ -91,6 +94,11 @@ def tile_list_linen_wear_pages_kernel(
             nc.sync.dma_start(tile[:], src[c * P : (c + 1) * P, :])
             return tile
 
+        def load_half(src, c, h, name):
+            tile = keep.tile([P, HALF], F32, name="%s%d%d" % (name, c, h))
+            nc.sync.dma_start(tile[:], src[c * P : (c + 1) * P, half_cols(h)])
+            return tile
+
         def interleave(dst, src):
             nc.scalar.copy(
                 dst.rearrange("p (c i t) -> p c t i", i=4, t=4),
@@ -123,8 +131,9 @@ def tile_list_linen_wear_pages_kernel(
         weights = [load_weights(0)]
         load_scale_rows(w2_s, w2_scales, nc.sync)
         words.append(load_table_words(1))
-        cycs = [load_rows(cyc, 0, "cyc")]
-        wgs_sb = load_rows(wgs, 0, "wgs")
+        cycs = {(0, h): load_half(cyc, 0, h, "cyc") for h in range(HALVES)}
+        weights.append(load_weights(1))
+        wgs_sb = [load_half(wgs, 0, 0, "wgs")]
         idx2 = load_list(offs2, "idx2")
         pages0 = []
 
@@ -142,8 +151,8 @@ def tile_list_linen_wear_pages_kernel(
             grouped = ring.tile([P, PASSES * 4 * P], BF16, name="w1_grouped", align_bytes=64)
             for a in range(PASSES):
                 interleave(grouped[:, a * 4 * P : (a + 1) * 4 * P], raw[a][:])
-            codes = ring.tile([P, PASSES * P], U32, name="w1_codes", align_bytes=64)
-            scales = ring.tile([P, PASSES * P], U8, name="w1_scales", align_bytes=64)
+            codes = ring.tile([P, PASSES * P], U32, name="w1_codes", align_bytes=64, bufs=3)
+            scales = ring.tile([P, PASSES * P], U8, name="w1_scales", align_bytes=64, bufs=3)
             nc.vector.quantize_mx(codes[:].bitcast(FP8X4), scales[:], grouped[:])
             return codes, scales
 
@@ -156,9 +165,9 @@ def tile_list_linen_wear_pages_kernel(
                 bank[:].rearrange("j b (q u e) -> j b u q e", u=2, e=2),
             )
 
-        def turn_back(turned):
+        def turn_back(turned, name):
             pairs = turned[:].rearrange("j b w -> j (b w)").bitcast(F32)
-            grouped = ring.tile([P, 4 * HALF], BF16, name="grouped", align_bytes=64)
+            grouped = keep.tile([P, 4 * HALF], BF16, name=name + "_grouped", tag=name + "_grouped", align_bytes=64)
             for g in range(2):
                 bank = psum.tile([P, 2, 2, P], F32, name="turn_b")
                 for b in range(2):
@@ -174,7 +183,7 @@ def tile_list_linen_wear_pages_kernel(
             return grouped
 
         def quantise_half(grouped, name):
-            codes = keep.tile([P, HALF], U32, name=name + "_codes", align_bytes=64)
+            codes = keep.tile([P, HALF], U32, name=name + "_codes", tag=name + "_codes", align_bytes=64)
             scales = keep.tile([P, HALF], U8, name=name + "_scales", align_bytes=64)
             nc.vector.quantize_mx(codes[:].bitcast(FP8X4), scales[:], grouped[:])
             return codes, scales
@@ -191,63 +200,76 @@ def tile_list_linen_wear_pages_kernel(
             nc.vector.quantize_mx(w3_codes[:, cols].bitcast(FP8X4), w3_scales[:, cols], grouped[:])
 
         h_turned = [keep.tile([P, 4, H], BF16, name="h_turned%d" % h) for h in range(HALVES)]
-        w1_q = quantise_w1(0)
-        for c in range(SLICES):
-            if c + 1 < SLICES:
-                weights.append(load_weights(c + 1))
-            page_c = load_rows(page0, c, "page0_")
-            pages0.append(page_c)
-            if c + 1 < SLICES:
-                cycs.append(load_rows(cyc, c + 1, "cyc"))
-            w1_codes, w1_scales = w1_q
+        w1_q = [quantise_w1(0), quantise_w1(1)]
+
+        def state(c, h):
+            w1_codes, w1_scales = w1_q[c]
             w2c = weights[c][1]
-            cyc_c = cycs[c]
             cols = slice(c * P, (c + 1) * P)
-            h_c = ring.tile([P, S], F32, name="h_c")
-            prods = []
-            sums = []
-            for h in range(HALVES):
-                sum_a = psum.tile([P, HALF], F32, name="sum_a")
-                sum_b = psum.tile([P, HALF], F32, name="sum_b")
-                for a in range(PASSES):
-                    nc.tensor.matmul_mx(
-                        sum_a[:],
-                        lhsT=w1_codes[:, a * P : (a + 1) * P].bitcast(FP8X4),
-                        lhsT_scale=w1_scales[:, a * P : (a + 1) * P],
-                        rhs=v_codes[a][h][:].bitcast(FP8X4),
-                        rhs_scale=v_scales[4 * a :, half_cols(h)],
-                        start=(a == 0),
-                        stop=(a == PASSES - 1),
-                    )
-                for a in range(PASSES):
-                    nc.tensor.matmul_mx(
-                        sum_b[:],
-                        lhsT=w2c[:, a, :].bitcast(FP8X4),
-                        lhsT_scale=w2_s[4 * a :, cols],
-                        rhs=v_codes[a][h][:].bitcast(FP8X4),
-                        rhs_scale=v_scales[4 * a :, half_cols(h)],
-                        start=(a == 0),
-                        stop=(a == PASSES - 1),
-                    )
-                squashed = ring.tile([P, HALF], F32, name="squashed", tag="ring_a", bufs=4)
-                nc.scalar.activation(squashed[:], sum_a[:], TANH)
-                prod = ring.tile([P, HALF], F32, name="prod", tag="ring_b", bufs=4)
-                nc.vector.scalar_tensor_tensor(
-                    prod[:], squashed[:], gain_c[:, c : c + 1], cyc_c[:, half_cols(h)], MULT, MULT
+            sum_a = psum.tile([P, HALF], F32, name="sum_a")
+            sum_b = psum.tile([P, HALF], F32, name="sum_b")
+            for a in range(PASSES):
+                nc.tensor.matmul_mx(
+                    sum_a[:],
+                    lhsT=w1_codes[:, a * P : (a + 1) * P].bitcast(FP8X4),
+                    lhsT_scale=w1_scales[:, a * P : (a + 1) * P],
+                    rhs=v_codes[a][h][:].bitcast(FP8X4),
+                    rhs_scale=v_scales[4 * a :, half_cols(h)],
+                    start=(a == 0),
+                    stop=(a == PASSES - 1),
                 )
-                prods.append(prod)
-                sums.append(sum_b)
-            for h in range(HALVES):
-                nc.vector.scalar_tensor_tensor(
-                    h_c[:, half_cols(h)], sums[h][:], gain_c[:, c : c + 1], prods[h][:], MULT, ADD
+            for a in range(PASSES):
+                nc.tensor.matmul_mx(
+                    sum_b[:],
+                    lhsT=w2c[:, a, :].bitcast(FP8X4),
+                    lhsT_scale=w2_s[4 * a :, cols],
+                    rhs=v_codes[a][h][:].bitcast(FP8X4),
+                    rhs_scale=v_scales[4 * a :, half_cols(h)],
+                    start=(a == 0),
+                    stop=(a == PASSES - 1),
                 )
-            if c + 1 < SLICES:
-                w1_q = quantise_w1(c + 1)
-            if c > 0:
+            squashed = ring.tile([P, HALF], F32, name="squashed", tag="ring_a", bufs=4)
+            nc.scalar.activation(squashed[:], sum_a[:], TANH)
+            prod = ring.tile([P, HALF], F32, name="prod", tag="ring_b", bufs=4)
+            factors = cycs[c, h][:]
+            if c == 0:
+                nc.vector.scalar_tensor_tensor(prod[:], squashed[:], gain_c[:, c : c + 1], factors, MULT, MULT)
+            else:
+                nc.scalar.activation(factors, factors, COPY, scale=gain_c[:, c : c + 1])
+                nc.gpsimd.tensor_tensor(prod[:], squashed[:], factors, MULT)
+            new = ring.tile([P, HALF], F32, name="new", bufs=4)
+            nc.vector.scalar_tensor_tensor(new[:], sum_b[:], gain_c[:, c : c + 1], prod[:], MULT, ADD)
+            return new
+
+        def put(c, h, new):
+            placed = cycs[units[(units.index((c, h)) + 1) % len(units)]]
+            engine = nc.vector if (c, h) == units[0] else nc.gpsimd
+            engine.tensor_tensor(placed[:], new[:], wgs_sb[h][:], MULT)
+            nc.vector.tensor_copy(pages0[c][:].indirect(half_list(idx2, h)), placed[:])
+            turn_rows(new[:], h_turned[h], c)
+
+        units = [(c, h) for c in range(SLICES) for h in range(HALVES)]
+        pending = None
+        for c, h in units:
+            if h == 0:
+                pages0.append(load_rows(page0, c, "page0_"))
+                if c + 1 < SLICES:
+                    cycs[c + 1, 0] = load_half(cyc, c + 1, 0, "cyc")
+                if c + 2 < SLICES:
+                    weights.append(load_weights(c + 2))
+                if c == 0:
+                    wgs_sb.append(load_half(wgs, 0, 1, "wgs"))
+                if c + 1 < SLICES:
+                    cycs[c + 1, 1] = load_half(cyc, c + 1, 1, "cyc")
+            new = state(c, h)
+            if h == 1 and c + 2 < SLICES:
+                w1_q.append(quantise_w1(c + 2))
+            if h == 1 and c > 0:
                 quantise_w3(c - 1)
-            nc.vector.tensor_tensor(page_c[:].indirect(idx2[:]), h_c[:], wgs_sb[:], MULT)
-            for h in range(HALVES):
-                turn_rows(h_c[:, half_cols(h)], h_turned[h], c)
+            if pending is not None:
+                put(*pending)
+            pending = (c, h, new)
+        put(*pending)
 
         w4_codes = keep.tile([P, 2 * N], U8, name="w4_codes", align_bytes=64)
         nc.sync.dma_start(w4_codes[:].bitcast(I32), w4_words[0].bitcast(I32))
@@ -263,28 +285,32 @@ def tile_list_linen_wear_pages_kernel(
             if nb == 1:
                 idx3 = load_list(offs3, "idx3")
 
-        h_grouped = [turn_back(h_turned[h]) for h in range(HALVES)]
+        h_grouped = [turn_back(h_turned[h], "h%d" % h) for h in range(HALVES)]
 
-        def recall(h):
-            turned = keep.tile([P, 4, H], BF16, name="x_turned%d" % h)
-            fetched = {}
-            for step in range(SLICES + 1):
-                if step < SLICES:
-                    c = step
-                    fetched[c] = ring.tile([P, HALF], F32, name="fetched", tag="ring_a", bufs=4)
-                    nc.vector.tensor_copy(fetched[c][:], pages0[c][:].indirect(half_list(idx3, h)))
-                if step > 0:
-                    c = step - 1
-                    floored = ring.tile([P, HALF], F32, name="floored", tag="ring_b", bufs=4)
-                    nc.vector.tensor_scalar(floored[:], fetched[c][:], lo_c[:, c : c + 1], None, MAX)
-                    turn_rows(floored[:], turned, c)
-            return turned
+        x_turned = [keep.tile([P, 4, H], BF16, name="x_turned%d" % h) for h in range(HALVES)]
 
-        x_turned = recall(0)
+        def recall(c, h, fetched):
+            nc.vector.tensor_copy(fetched[:], pages0[c][:].indirect(half_list(idx3, h)))
+            floored = ring.tile([P, HALF], F32, name="floored", tag="ring_b", bufs=4)
+            nc.gpsimd.tensor_scalar(floored[:], fetched[:], F32_MAX, lo_c[:, c : c + 1], MIN, MAX)
+            turn_rows(floored[:], x_turned[h], c)
+
+        def ring_tile():
+            return ring.tile([P, HALF], F32, name="fetched", tag="ring_a", bufs=4)
+
+        def tile_on(tag):
+            return keep.tile([P, HALF], F32, name="fetched_last", tag=tag, align_bytes=64)
+
+        for c in range(SLICES - 1):
+            recall(c, 0, ring_tile())
+        recall(SLICES - 1, 0, tile_on("h1_codes"))
         h_q = [quantise_half(h_grouped[h], "h%d" % h) for h in range(HALVES)]
-        x_grouped = [turn_back(x_turned)]
-        x_grouped.append(turn_back(recall(1)))
-        x_q = [quantise_half(x_grouped[0], "x0")]
+        x_grouped = turn_back(x_turned[0], "x0")
+        for c in range(SLICES - 1):
+            recall(c, 1, ring_tile())
+        x_q = [quantise_half(x_grouped, "x0")]
+        recall(SLICES - 1, 1, tile_on("x0_grouped"))
+        x_grouped = turn_back(x_turned[1], "h0")
 
         def place(nb, h):
             cols = slice(nb * P, (nb + 1) * P)
@@ -317,7 +343,7 @@ def tile_list_linen_wear_pages_kernel(
             )
 
         place(0, 0)
-        x_q.append(quantise_half(x_grouped[1], "x1"))
+        x_q.append(quantise_half(x_grouped, "x1"))
         for nb in range(BLOCKS):
             if nb + 1 < BLOCKS:
                 place(nb + 1, 0)

@@ -29,6 +29,7 @@ BLOCKS = N // P
 HALF = 512
 HALVES = S // HALF
 LIST_COLS = HALF // 16
+BANKS = {"turn": 4, "sum_a": 2}
 W3_PART = N // (SLICES - 1)
 
 
@@ -77,17 +78,21 @@ def tile_list_linen_wear_pages_kernel(
             cols = slice(c * P, (c + 1) * P)
             raw = []
             for a in range(PASSES):
-                tile = ring.tile([P, 4, P], F32, name="w1_raw%d" % a)
+                tile = keep.tile([P, 4, P], F32, name="w1_raw%d%d" % (c, a))
                 nc.sync.dma_start(
                     tile[:], w1[512 * a : 512 * (a + 1), cols].rearrange("(p j) r -> p j r", j=4)
                 )
                 raw.append(tile)
+            return raw
+
+        def load_w2(c):
+            cols = slice(c * P, (c + 1) * P)
             w2c = keep.tile([P, PASSES, P], I32, name="w2_codes%d" % c, align_bytes=64)
             nc.sync.dma_start(
                 w2c[:],
                 w2_words[:, :, cols, :].rearrange("a p n t -> p a (n t)").bitcast(I32),
             )
-            return raw, w2c
+            return w2c
 
         def load_rows(src, c, name):
             tile = keep.tile([P, src.shape[1]], F32, name="%s%d" % (name, c))
@@ -98,6 +103,14 @@ def tile_list_linen_wear_pages_kernel(
             tile = keep.tile([P, HALF], F32, name="%s%d%d" % (name, c, h))
             nc.sync.dma_start(tile[:], src[c * P : (c + 1) * P, half_cols(h)])
             return tile
+
+        def load_w3(part):
+            cols = slice(part * W3_PART, (part + 1) * W3_PART)
+            raw = shared.tile(
+                [P, 4, W3_PART], F32, name="w3_raw%d" % part, offset=PASSES * T * 4 + T + part * 16 * W3_PART
+            )
+            nc.sync.dma_start(raw[:], w3[:, cols].rearrange("(p j) n -> p j n", j=4))
+            return raw
 
         def interleave(dst, src):
             nc.scalar.copy(
@@ -120,7 +133,7 @@ def tile_list_linen_wear_pages_kernel(
         ident = keep.tile([P, P], F32, name="ident")
         make_identity(nc, ident[:])
         w4_s = scale_tile(N, "w4_s", nc.gpsimd)
-        turned_vectors = psum.tile([P, P], F32, name="turn_a")
+        turned_vectors = psum.tile([P, P], F32, name="turn_v", tag="turn", bufs=BANKS["turn"])
         nc.tensor.transpose(turned_vectors[:], vectors[:], ident[:])
         per_row = keep.tile([P, 2 * SLICES], F32, name="per_row")
         nc.scalar.copy(per_row[:], turned_vectors[:, 0 : 2 * SLICES])
@@ -129,13 +142,29 @@ def tile_list_linen_wear_pages_kernel(
 
         words = [load_table_words(0)]
         weights = [load_weights(0)]
+        w2_codes = [load_w2(0)]
         load_scale_rows(w2_s, w2_scales, nc.sync)
         words.append(load_table_words(1))
-        cycs = {(0, h): load_half(cyc, 0, h, "cyc") for h in range(HALVES)}
+        cycs = {(0, 0): load_half(cyc, 0, 0, "cyc")}
         weights.append(load_weights(1))
+        cycs[0, 1] = load_half(cyc, 0, 1, "cyc")
         wgs_sb = [load_half(wgs, 0, 0, "wgs")]
         idx2 = load_list(offs2, "idx2")
-        pages0 = []
+        pages0 = [load_rows(page0, 0, "page0_")]
+        cycs[1, 0] = load_half(cyc, 1, 0, "cyc")
+        w2_codes.append(load_w2(1))
+        weights.append(load_weights(2))
+        wgs_sb.append(load_half(wgs, 0, 1, "wgs"))
+        cycs[1, 1] = load_half(cyc, 1, 1, "cyc")
+        w2_codes.append(load_w2(2))
+        weights.append(load_weights(3))
+        w2_codes.append(load_w2(3))
+        for c in range(1, SLICES):
+            pages0.append(load_rows(page0, c, "page0_"))
+            if c + 1 < SLICES:
+                for h in range(HALVES):
+                    cycs[c + 1, h] = load_half(cyc, c + 1, h, "cyc")
+        w3_raw = [load_w3(part) for part in range(SLICES - 1)]
 
         v_codes = [[None] * HALVES for a in range(PASSES)]
         v_scales = keep.tile([P, S], U8, name="v_scales", align_bytes=64)
@@ -147,7 +176,7 @@ def tile_list_linen_wear_pages_kernel(
                 v_codes[a][h] = picked
 
         def quantise_w1(c):
-            raw = weights[c][0]
+            raw = weights[c]
             grouped = ring.tile([P, PASSES * 4 * P], BF16, name="w1_grouped", align_bytes=64)
             for a in range(PASSES):
                 interleave(grouped[:, a * 4 * P : (a + 1) * 4 * P], raw[a][:])
@@ -156,8 +185,8 @@ def tile_list_linen_wear_pages_kernel(
             nc.vector.quantize_mx(codes[:].bitcast(FP8X4), scales[:], grouped[:])
             return codes, scales
 
-        def turn_rows(values, turned, c):
-            bank = psum.tile([P, 4, P], F32, name="turn_a")
+        def turn_rows(values, turned, c, tag="turn"):
+            bank = psum.tile([P, 4, P], F32, name="turn_a", tag=tag, bufs=BANKS[tag])
             for b in range(4):
                 nc.tensor.transpose(bank[:, b, :], values[:, b * P : (b + 1) * P], ident[:])
             nc.scalar.copy(
@@ -169,7 +198,7 @@ def tile_list_linen_wear_pages_kernel(
             pairs = turned[:].rearrange("j b w -> j (b w)").bitcast(F32)
             grouped = keep.tile([P, 4 * HALF], BF16, name=name + "_grouped", tag=name + "_grouped", align_bytes=64)
             for g in range(2):
-                bank = psum.tile([P, 2, 2, P], F32, name="turn_b")
+                bank = psum.tile([P, 2, 2, P], F32, name="turn_b", tag="turn", bufs=BANKS["turn"])
                 for b in range(2):
                     for u in range(2):
                         first = (2 * (2 * g + b) + u) * P
@@ -182,31 +211,20 @@ def tile_list_linen_wear_pages_kernel(
                 )
             return grouped
 
-        def quantise_half(grouped, name):
-            codes = keep.tile([P, HALF], U32, name=name + "_codes", tag=name + "_codes", align_bytes=64)
+        def quantise_half(grouped, name, tag):
+            codes = keep.tile([P, HALF], U32, name=name + "_codes", tag=tag, align_bytes=64)
             scales = keep.tile([P, HALF], U8, name=name + "_scales", align_bytes=64)
             nc.vector.quantize_mx(codes[:].bitcast(FP8X4), scales[:], grouped[:])
             return codes, scales
 
-        w3_codes = keep.tile([P, N], U32, name="w3_codes", align_bytes=64)
-        w3_scales = keep.tile([P, N], U8, name="w3_scales", align_bytes=64)
-
-        def quantise_w3(part):
-            cols = slice(part * W3_PART, (part + 1) * W3_PART)
-            raw = ring.tile([P, 4, W3_PART], F32, name="w3_raw")
-            nc.sync.dma_start(raw[:], w3[:, cols].rearrange("(p j) n -> p j n", j=4))
-            grouped = ring.tile([P, 4 * W3_PART], BF16, name="w3_grouped", align_bytes=64)
-            interleave(grouped[:], raw[:])
-            nc.vector.quantize_mx(w3_codes[:, cols].bitcast(FP8X4), w3_scales[:, cols], grouped[:])
-
-        h_turned = [keep.tile([P, 4, H], BF16, name="h_turned%d" % h) for h in range(HALVES)]
-        w1_q = [quantise_w1(0), quantise_w1(1)]
+        h_turned = [keep.tile([P, 4, H], BF16, name="h_turned%d" % h, tag="turned%d" % h) for h in range(HALVES)]
+        w1_q = [quantise_w1(0)]
 
         def state(c, h):
             w1_codes, w1_scales = w1_q[c]
-            w2c = weights[c][1]
+            w2c = w2_codes[c]
             cols = slice(c * P, (c + 1) * P)
-            sum_a = psum.tile([P, HALF], F32, name="sum_a")
+            sum_a = psum.tile([P, HALF], F32, name="sum_a", tag="sum_a")
             sum_b = psum.tile([P, HALF], F32, name="sum_b")
             for a in range(PASSES):
                 nc.tensor.matmul_mx(
@@ -228,48 +246,42 @@ def tile_list_linen_wear_pages_kernel(
                     start=(a == 0),
                     stop=(a == PASSES - 1),
                 )
-            squashed = ring.tile([P, HALF], F32, name="squashed", tag="ring_a", bufs=4)
+            squashed = ring.tile([P, HALF], F32, name="squashed", tag="ring_a", bufs=8)
             nc.scalar.activation(squashed[:], sum_a[:], TANH)
-            prod = ring.tile([P, HALF], F32, name="prod", tag="ring_b", bufs=4)
+            prod = squashed
             factors = cycs[c, h][:]
-            if c == 0:
+            if (c, h) == units[0]:
                 nc.vector.scalar_tensor_tensor(prod[:], squashed[:], gain_c[:, c : c + 1], factors, MULT, MULT)
             else:
                 nc.scalar.activation(factors, factors, COPY, scale=gain_c[:, c : c + 1])
                 nc.gpsimd.tensor_tensor(prod[:], squashed[:], factors, MULT)
-            new = ring.tile([P, HALF], F32, name="new", bufs=4)
+            new = ring.tile([P, HALF], F32, name="new", tag="new", bufs=8)
             nc.vector.scalar_tensor_tensor(new[:], sum_b[:], gain_c[:, c : c + 1], prod[:], MULT, ADD)
             return new
 
         def put(c, h, new):
-            placed = cycs[units[(units.index((c, h)) + 1) % len(units)]]
-            engine = nc.vector if (c, h) == units[0] else nc.gpsimd
+            u = units.index((c, h))
+            placed = cycs[units[u + 1]] if 0 < u < len(units) - 1 else cycs[units[0]]
+            engine = nc.vector if u < 2 else nc.gpsimd
             engine.tensor_tensor(placed[:], new[:], wgs_sb[h][:], MULT)
             nc.vector.tensor_copy(pages0[c][:].indirect(half_list(idx2, h)), placed[:])
-            turn_rows(new[:], h_turned[h], c)
+            states.append(new)
 
         units = [(c, h) for c in range(SLICES) for h in range(HALVES)]
-        pending = None
-        for c, h in units:
-            if h == 0:
-                pages0.append(load_rows(page0, c, "page0_"))
-                if c + 1 < SLICES:
-                    cycs[c + 1, 0] = load_half(cyc, c + 1, 0, "cyc")
-                if c + 2 < SLICES:
-                    weights.append(load_weights(c + 2))
-                if c == 0:
-                    wgs_sb.append(load_half(wgs, 0, 1, "wgs"))
-                if c + 1 < SLICES:
-                    cycs[c + 1, 1] = load_half(cyc, c + 1, 1, "cyc")
-            new = state(c, h)
+        states = []
+        put(0, 0, state(0, 0))
+        w1_q.append(quantise_w1(1))
+        new = state(0, 1)
+        for u in range(1, len(units)):
+            c, h = units[u]
+            following = state(*units[u + 1]) if u + 1 < len(units) else None
             if h == 1 and c + 2 < SLICES:
                 w1_q.append(quantise_w1(c + 2))
-            if h == 1 and c > 0:
-                quantise_w3(c - 1)
-            if pending is not None:
-                put(*pending)
-            pending = (c, h, new)
-        put(*pending)
+            put(c, h, new)
+            new = following
+        w3_grouped = keep.tile([P, 4 * N], BF16, name="w3_grouped", align_bytes=64)
+        for part in range(SLICES - 1):
+            interleave(w3_grouped[:, 4 * part * W3_PART : 4 * (part + 1) * W3_PART], w3_raw[part][:])
 
         w4_codes = keep.tile([P, 2 * N], U8, name="w4_codes", align_bytes=64)
         nc.sync.dma_start(w4_codes[:].bitcast(I32), w4_words[0].bitcast(I32))
@@ -285,36 +297,42 @@ def tile_list_linen_wear_pages_kernel(
             if nb == 1:
                 idx3 = load_list(offs3, "idx3")
 
+        for u, (c, h) in enumerate(units):
+            turn_rows(states[u][:], h_turned[h], c, "sum_a")
         h_grouped = [turn_back(h_turned[h], "h%d" % h) for h in range(HALVES)]
 
-        x_turned = [keep.tile([P, 4, H], BF16, name="x_turned%d" % h) for h in range(HALVES)]
+        x_turned = [keep.tile([P, 4, H], BF16, name="x_turned%d" % h, tag="turned%d" % h) for h in range(HALVES)]
 
         def recall(c, h, fetched):
             nc.vector.tensor_copy(fetched[:], pages0[c][:].indirect(half_list(idx3, h)))
             floored = ring.tile([P, HALF], F32, name="floored", tag="ring_b", bufs=4)
             nc.gpsimd.tensor_scalar(floored[:], fetched[:], F32_MAX, lo_c[:, c : c + 1], MIN, MAX)
-            turn_rows(floored[:], x_turned[h], c)
+            return floored
 
         def ring_tile():
-            return ring.tile([P, HALF], F32, name="fetched", tag="ring_a", bufs=4)
+            return ring.tile([P, HALF], F32, name="fetched", tag="ring_a", bufs=8)
 
-        def tile_on(tag):
-            return keep.tile([P, HALF], F32, name="fetched_last", tag=tag, align_bytes=64)
-
-        for c in range(SLICES - 1):
-            recall(c, 0, ring_tile())
-        recall(SLICES - 1, 0, tile_on("h1_codes"))
-        h_q = [quantise_half(h_grouped[h], "h%d" % h) for h in range(HALVES)]
+        h_q = [quantise_half(h_grouped[0], "h0", "h0_codes")]
+        for c in range(SLICES):
+            last = c == SLICES - 1
+            fetched = keep.tile([P, HALF], F32, name="held", tag="w3_codes", align_bytes=64) if last else ring_tile()
+            turn_rows(recall(c, 0, fetched)[:], x_turned[0], c)
         x_grouped = turn_back(x_turned[0], "x0")
-        for c in range(SLICES - 1):
-            recall(c, 1, ring_tile())
-        x_q = [quantise_half(x_grouped, "x0")]
-        recall(SLICES - 1, 1, tile_on("x0_grouped"))
-        x_grouped = turn_back(x_turned[1], "h0")
+        floors = [recall(c, 1, ring_tile()) for c in range(SLICES)]
+        w3_codes = keep.tile([P, N], U32, name="w3_codes", tag="w3_codes", align_bytes=64)
+        w3_scales = keep.tile([P, N], U8, name="w3_scales", align_bytes=64)
+        for first, last in ((0, 512), (512, N)):
+            nc.vector.quantize_mx(
+                w3_codes[:, first:last].bitcast(FP8X4),
+                w3_scales[:, first:last],
+                w3_grouped[:, 4 * first : 4 * last],
+            )
+        x_q = [quantise_half(x_grouped, "x0", "x0_codes")]
+        h_q.append(quantise_half(h_grouped[1], "h1", "x0_grouped"))
 
-        def place(nb, h):
+        def fresh(nb, h):
             cols = slice(nb * P, (nb + 1) * P)
-            sum_2 = psum.tile([P, HALF], F32, name="sum_b")
+            sum_2 = psum.tile([P, HALF], F32, name="sum_2", tag="turn", bufs=BANKS["turn"])
             nc.tensor.matmul_mx(
                 sum_2[:],
                 lhsT=w4_codes[:, 2 * nb * P : 2 * (nb + 1) * P].bitcast(FP4X4),
@@ -324,9 +342,13 @@ def tile_list_linen_wear_pages_kernel(
                 start=True,
                 stop=True,
             )
-            y2 = ring.tile([P, HALF], F32, name="y2", tag="ring_a", bufs=4)
+            y2 = ring.tile([P, HALF], F32, name="y2", tag="ring_a", bufs=8)
             nc.scalar.copy(y2[:], sum_2[:])
-            sum_1 = psum.tile([P, HALF], F32, name="sum_a")
+            return y2
+
+        def place(nb, h, y2):
+            cols = slice(nb * P, (nb + 1) * P)
+            sum_1 = psum.tile([P, HALF], F32, name="sum_1", tag="sum_a")
             nc.tensor.matmul_mx(
                 sum_1[:],
                 lhsT=w3_codes[:, cols].bitcast(FP8X4),
@@ -336,16 +358,23 @@ def tile_list_linen_wear_pages_kernel(
                 start=True,
                 stop=True,
             )
-            y = ring.tile([P, HALF], F32, name="y", tag="ring_b", bufs=4)
+            y = ring.tile([P, HALF], F32, name="y", tag="new", bufs=8)
             nc.vector.tensor_tensor(y[:], sum_1[:], y2[:], MAX)
             nc.vector.tensor_tensor(
                 pages[nb][:].indirect(half_list(idx4, h)), y[:], wgo_sb[:, half_cols(h)], MULT
             )
 
-        place(0, 0)
-        x_q.append(quantise_half(x_grouped, "x1"))
+        place(0, 0, fresh(0, 0))
+        place(1, 0, fresh(1, 0))
+        early = [fresh(nb, 0) for nb in (2, 3)]
+        for c in range(SLICES):
+            turn_rows(floors[c][:], x_turned[1], c, "sum_a")
+        x_grouped = turn_back(x_turned[1], "h0")
+        place(2, 0, early[0])
+        x_q.append(quantise_half(x_grouped, "x1", "x1_codes"))
+        place(3, 0, early[1])
         for nb in range(BLOCKS):
-            if nb + 1 < BLOCKS:
-                place(nb + 1, 0)
-            place(nb, 1)
+            place(nb, 1, fresh(nb, 1))
             nc.sync.dma_start(out[nb * P : (nb + 1) * P, :], pages[nb][:])
+            if nb + 4 < BLOCKS:
+                place(nb + 4, 0, fresh(nb + 4, 0))

@@ -30,6 +30,8 @@ HALF = 512
 HALVES = S // HALF
 LIST_COLS = HALF // 16
 BANKS = {"turn": 4, "sum_a": 2}
+VECTOR_SUMS = 2
+LATE_TURN = 5
 W3_PART = N // (SLICES - 1)
 
 
@@ -100,7 +102,8 @@ def tile_list_linen_wear_pages_kernel(
             return tile
 
         def load_half(src, c, h, name):
-            tile = keep.tile([P, HALF], F32, name="%s%d%d" % (name, c, h))
+            label = "%s%d%d" % (name, c, h)
+            tile = keep.tile([P, HALF], F32, name=label, tag=label, align_bytes=64)
             nc.sync.dma_start(tile[:], src[c * P : (c + 1) * P, half_cols(h)])
             return tile
 
@@ -151,17 +154,17 @@ def tile_list_linen_wear_pages_kernel(
         wgs_sb = [load_half(wgs, 0, 0, "wgs")]
         idx2 = load_list(offs2, "idx2")
         pages0 = [load_rows(page0, 0, "page0_")]
-        cycs[1, 0] = load_half(cyc, 1, 0, "cyc")
         w2_codes.append(load_w2(1))
+        cycs[1, 0] = load_half(cyc, 1, 0, "cyc")
         weights.append(load_weights(2))
+        idx3 = load_list(offs3, "idx3")
         wgs_sb.append(load_half(wgs, 0, 1, "wgs"))
         cycs[1, 1] = load_half(cyc, 1, 1, "cyc")
-        w2_codes.append(load_w2(2))
         weights.append(load_weights(3))
-        w2_codes.append(load_w2(3))
         for c in range(1, SLICES):
             pages0.append(load_rows(page0, c, "page0_"))
             if c + 1 < SLICES:
+                w2_codes.append(load_w2(c + 1))
                 for h in range(HALVES):
                     cycs[c + 1, h] = load_half(cyc, c + 1, h, "cyc")
         w3_raw = [load_w3(part) for part in range(SLICES - 1)]
@@ -180,8 +183,8 @@ def tile_list_linen_wear_pages_kernel(
             grouped = ring.tile([P, PASSES * 4 * P], BF16, name="w1_grouped", align_bytes=64)
             for a in range(PASSES):
                 interleave(grouped[:, a * 4 * P : (a + 1) * 4 * P], raw[a][:])
-            codes = ring.tile([P, PASSES * P], U32, name="w1_codes", align_bytes=64, bufs=3)
-            scales = ring.tile([P, PASSES * P], U8, name="w1_scales", align_bytes=64, bufs=3)
+            codes = ring.tile([P, PASSES * P], U32, name="w1_codes", align_bytes=64, bufs=4)
+            scales = ring.tile([P, PASSES * P], U8, name="w1_scales", align_bytes=64, bufs=4)
             nc.vector.quantize_mx(codes[:].bitcast(FP8X4), scales[:], grouped[:])
             return codes, scales
 
@@ -194,11 +197,11 @@ def tile_list_linen_wear_pages_kernel(
                 bank[:].rearrange("j b (q u e) -> j b u q e", u=2, e=2),
             )
 
-        def turn_back(turned, name):
+        def turn_back(turned, name, tag="turn"):
             pairs = turned[:].rearrange("j b w -> j (b w)").bitcast(F32)
             grouped = keep.tile([P, 4 * HALF], BF16, name=name + "_grouped", tag=name + "_grouped", align_bytes=64)
             for g in range(2):
-                bank = psum.tile([P, 2, 2, P], F32, name="turn_b", tag="turn", bufs=BANKS["turn"])
+                bank = psum.tile([P, 2, 2, P], F32, name="turn_b", tag=tag, bufs=BANKS[tag])
                 for b in range(2):
                     for u in range(2):
                         first = (2 * (2 * g + b) + u) * P
@@ -225,7 +228,7 @@ def tile_list_linen_wear_pages_kernel(
             w2c = w2_codes[c]
             cols = slice(c * P, (c + 1) * P)
             sum_a = psum.tile([P, HALF], F32, name="sum_a", tag="sum_a")
-            sum_b = psum.tile([P, HALF], F32, name="sum_b")
+            sum_b = psum.tile([P, HALF], F32, name="sum_b", tag="sum_b")
             for a in range(PASSES):
                 nc.tensor.matmul_mx(
                     sum_a[:],
@@ -246,39 +249,48 @@ def tile_list_linen_wear_pages_kernel(
                     start=(a == 0),
                     stop=(a == PASSES - 1),
                 )
-            squashed = ring.tile([P, HALF], F32, name="squashed", tag="ring_a", bufs=8)
+            squashed = ring.tile([P, HALF], F32, name="squashed", tag="ring_a", bufs=7)
             nc.scalar.activation(squashed[:], sum_a[:], TANH)
-            prod = squashed
+            u = units.index((c, h))
+            prod = squashed if u < VECTOR_SUMS else product
             factors = cycs[c, h][:]
             if (c, h) == units[0]:
                 nc.vector.scalar_tensor_tensor(prod[:], squashed[:], gain_c[:, c : c + 1], factors, MULT, MULT)
             else:
                 nc.scalar.activation(factors, factors, COPY, scale=gain_c[:, c : c + 1])
                 nc.gpsimd.tensor_tensor(prod[:], squashed[:], factors, MULT)
-            new = ring.tile([P, HALF], F32, name="new", tag="new", bufs=8)
-            nc.vector.scalar_tensor_tensor(new[:], sum_b[:], gain_c[:, c : c + 1], prod[:], MULT, ADD)
+            new = ring.tile([P, HALF], F32, name="new", tag="new", bufs=7)
+            if u < VECTOR_SUMS:
+                nc.vector.scalar_tensor_tensor(new[:], sum_b[:], gain_c[:, c : c + 1], prod[:], MULT, ADD)
+            else:
+                nc.scalar.activation(new[:], sum_b[:], COPY, scale=gain_c[:, c : c + 1])
+                nc.gpsimd.tensor_tensor(new[:], new[:], prod[:], ADD)
             return new
 
         def put(c, h, new):
             u = units.index((c, h))
-            placed = cycs[units[u + 1]] if 0 < u < len(units) - 1 else cycs[units[0]]
-            engine = nc.vector if u < 2 else nc.gpsimd
+            if u == len(units) - 1:
+                placed = keep.tile([P, HALF], F32, name="placed_last", tag="late")
+            else:
+                placed = cycs[c, h]
+            engine = nc.vector if u < VECTOR_SUMS else nc.gpsimd
             engine.tensor_tensor(placed[:], new[:], wgs_sb[h][:], MULT)
             nc.vector.tensor_copy(pages0[c][:].indirect(half_list(idx2, h)), placed[:])
-            states.append(new)
+            if u < VECTOR_SUMS:
+                waiting.append((new, c, h))
+            else:
+                turn_rows(new[:], h_turned[h], c)
+            if u == LATE_TURN:
+                for state_tile, its_c, its_h in waiting:
+                    turn_rows(state_tile[:], h_turned[its_h], its_c)
 
         units = [(c, h) for c in range(SLICES) for h in range(HALVES)]
-        states = []
-        put(0, 0, state(0, 0))
-        w1_q.append(quantise_w1(1))
-        new = state(0, 1)
-        for u in range(1, len(units)):
-            c, h = units[u]
-            following = state(*units[u + 1]) if u + 1 < len(units) else None
-            if h == 1 and c + 2 < SLICES:
-                w1_q.append(quantise_w1(c + 2))
-            put(c, h, new)
-            new = following
+        waiting = []
+        product = keep.tile([P, HALF], F32, name="product", tag="product")
+        for c, h in units:
+            put(c, h, state(c, h))
+            if len(w1_q) < SLICES:
+                w1_q.append(quantise_w1(len(w1_q)))
         w3_grouped = keep.tile([P, 4 * N], BF16, name="w3_grouped", align_bytes=64)
         for part in range(SLICES - 1):
             interleave(w3_grouped[:, 4 * part * W3_PART : 4 * (part + 1) * W3_PART], w3_raw[part][:])
@@ -294,45 +306,36 @@ def tile_list_linen_wear_pages_kernel(
             page = shared.tile([P, T2], F32, name="page1_%d" % nb, offset=nb * T2 * 4)
             nc.sync.dma_start(page[:], page1[nb * P : (nb + 1) * P, :])
             pages.append(page)
-            if nb == 1:
-                idx3 = load_list(offs3, "idx3")
 
-        for u, (c, h) in enumerate(units):
-            turn_rows(states[u][:], h_turned[h], c, "sum_a")
-        h_grouped = [turn_back(h_turned[h], "h%d" % h) for h in range(HALVES)]
+        h_q = [quantise_half(turn_back(h_turned[0], "h0"), "h0", "wgs01")]
 
-        x_turned = [keep.tile([P, 4, H], BF16, name="x_turned%d" % h, tag="turned%d" % h) for h in range(HALVES)]
+        def recall(c, h, fetched, floored):
+            nc.vector.tensor_copy(fetched, pages0[c][:].indirect(half_list(idx3, h)))
+            nc.gpsimd.tensor_scalar(floored, fetched, F32_MAX, lo_c[:, c : c + 1], MIN, MAX)
 
-        def recall(c, h, fetched):
-            nc.vector.tensor_copy(fetched[:], pages0[c][:].indirect(half_list(idx3, h)))
-            floored = ring.tile([P, HALF], F32, name="floored", tag="ring_b", bufs=4)
-            nc.gpsimd.tensor_scalar(floored[:], fetched[:], F32_MAX, lo_c[:, c : c + 1], MIN, MAX)
-            return floored
+        def quantise_w3(first, last, tag):
+            codes = keep.tile([P, last - first], U32, name="w3_codes", tag=tag, align_bytes=64)
+            scales = keep.tile([P, last - first], U8, name="w3_scales%d" % first, align_bytes=64)
+            nc.vector.quantize_mx(codes[:].bitcast(FP8X4), scales[:], w3_grouped[:, 4 * first : 4 * last])
+            return [(codes[:, n : n + P], scales[:, n : n + P]) for n in range(0, last - first, P)]
 
-        def ring_tile():
-            return ring.tile([P, HALF], F32, name="fetched", tag="ring_a", bufs=8)
-
-        h_q = [quantise_half(h_grouped[0], "h0", "h0_codes")]
+        x_turned = keep.tile([P, 4, H], BF16, name="x_turned0")
+        floored = keep.tile([P, SLICES, HALF], F32, name="floored", tag="product")
+        for c, tag in enumerate(("cyc00", "cyc01", "cyc10", "w3_codes")):
+            fetched = keep.tile([P, HALF], F32, name="fetched", tag=tag, align_bytes=64)
+            recall(c, 0, fetched[:], floored[:, c, :])
+            turn_rows(floored[:, c, :], x_turned, c)
+        x_grouped = turn_back(x_turned, "x0")
+        late = keep.tile([P, SLICES, HALF], F32, name="late", tag="late")
         for c in range(SLICES):
-            last = c == SLICES - 1
-            fetched = keep.tile([P, HALF], F32, name="held", tag="w3_codes", align_bytes=64) if last else ring_tile()
-            turn_rows(recall(c, 0, fetched)[:], x_turned[0], c)
-        x_grouped = turn_back(x_turned[0], "x0")
-        floors = [recall(c, 1, ring_tile()) for c in range(SLICES)]
-        w3_codes = keep.tile([P, N], U32, name="w3_codes", tag="w3_codes", align_bytes=64)
-        w3_scales = keep.tile([P, N], U8, name="w3_scales", align_bytes=64)
-        for first, last in ((0, 512), (512, N)):
-            nc.vector.quantize_mx(
-                w3_codes[:, first:last].bitcast(FP8X4),
-                w3_scales[:, first:last],
-                w3_grouped[:, 4 * first : 4 * last],
-            )
+            recall(c, 1, late[:, c, :], late[:, c, :])
+        w3_q = quantise_w3(0, HALF, "w3_codes")
         x_q = [quantise_half(x_grouped, "x0", "x0_codes")]
-        h_q.append(quantise_half(h_grouped[1], "h1", "x0_grouped"))
+        w3_q.extend(quantise_w3(HALF, N, "x0_grouped"))
 
-        def fresh(nb, h):
+        def fresh(nb, h, tag="turn"):
             cols = slice(nb * P, (nb + 1) * P)
-            sum_2 = psum.tile([P, HALF], F32, name="sum_2", tag="turn", bufs=BANKS["turn"])
+            sum_2 = psum.tile([P, HALF], F32, name="sum_2", tag=tag, bufs=BANKS[tag])
             nc.tensor.matmul_mx(
                 sum_2[:],
                 lhsT=w4_codes[:, 2 * nb * P : 2 * (nb + 1) * P].bitcast(FP4X4),
@@ -342,23 +345,23 @@ def tile_list_linen_wear_pages_kernel(
                 start=True,
                 stop=True,
             )
-            y2 = ring.tile([P, HALF], F32, name="y2", tag="ring_a", bufs=8)
+            y2 = ring.tile([P, HALF], F32, name="y2", tag="ring_a", bufs=7)
             nc.scalar.copy(y2[:], sum_2[:])
             return y2
 
-        def place(nb, h, y2):
-            cols = slice(nb * P, (nb + 1) * P)
-            sum_1 = psum.tile([P, HALF], F32, name="sum_1", tag="sum_a")
+        def place(nb, h, y2, tag="sum_a", y=None):
+            sum_1 = psum.tile([P, HALF], F32, name="sum_1", tag=tag)
             nc.tensor.matmul_mx(
                 sum_1[:],
-                lhsT=w3_codes[:, cols].bitcast(FP8X4),
-                lhsT_scale=w3_scales[:, cols],
+                lhsT=w3_q[nb][0].bitcast(FP8X4),
+                lhsT_scale=w3_q[nb][1],
                 rhs=x_q[h][0][:].bitcast(FP8X4),
                 rhs_scale=x_q[h][1][:],
                 start=True,
                 stop=True,
             )
-            y = ring.tile([P, HALF], F32, name="y", tag="new", bufs=8)
+            if y is None:
+                y = ring.tile([P, HALF], F32, name="y", tag="new", bufs=7)
             nc.vector.tensor_tensor(y[:], sum_1[:], y2[:], MAX)
             nc.vector.tensor_tensor(
                 pages[nb][:].indirect(half_list(idx4, h)), y[:], wgo_sb[:, half_cols(h)], MULT
@@ -366,15 +369,20 @@ def tile_list_linen_wear_pages_kernel(
 
         place(0, 0, fresh(0, 0))
         place(1, 0, fresh(1, 0))
-        early = [fresh(nb, 0) for nb in (2, 3)]
+        early = [fresh(nb, 0, "sum_a") for nb in (2, 3, 4)]
+        x_turned = keep.tile([P, 4, H], BF16, name="x_turned1", tag="turned0")
         for c in range(SLICES):
-            turn_rows(floors[c][:], x_turned[1], c, "sum_a")
-        x_grouped = turn_back(x_turned[1], "h0")
-        place(2, 0, early[0])
+            turn_rows(late[:, c, :], x_turned, c, "sum_a")
+        x_grouped = turn_back(x_turned, "h0")
+        h_grouped = turn_back(h_turned[1], "h1")
+        place(2, 0, early[0], "sum_b")
         x_q.append(quantise_half(x_grouped, "x1", "x1_codes"))
-        place(3, 0, early[1])
+        h_q.append(quantise_half(h_grouped, "h1", "h1_codes"))
+        held = keep.tile([P, HALF], F32, name="held_y", tag="h1_grouped", align_bytes=64)
+        place(3, 0, early[1], "sum_b", held)
+        place(4, 0, early[2])
         for nb in range(BLOCKS):
             place(nb, 1, fresh(nb, 1))
             nc.sync.dma_start(out[nb * P : (nb + 1) * P, :], pages[nb][:])
-            if nb + 4 < BLOCKS:
-                place(nb + 4, 0, fresh(nb + 4, 0))
+            if nb == 0:
+                place(5, 0, fresh(5, 0))

@@ -23,16 +23,23 @@ COPY = mybir.ActivationFunctionType.Copy
 F32_MAX = 3.4028234663852886e38
 
 P = 128
-PASSES = K // 512
+PACK = 4
+K_PASS = P * PACK
+PASSES = K // K_PASS
+QUADRANT = 32
 SLICES = H // P
 BLOCKS = N // P
 HALF = 512
 HALVES = S // HALF
 LIST_COLS = HALF // 16
-BANKS = {"turn": 4, "sum_a": 2}
-VECTOR_SUMS = 2
-LATE_TURN = 5
-W3_PART = N // (SLICES - 1)
+W3_PARTS = 3
+W3_PART = N // W3_PARTS
+BANKS = {"turn": 4, "sum_a": 2, "sum_b": 2}
+FROM_PSUM_BUFS = 7
+STATE_BUFS = 6
+
+LANDED_AT = PASSES * T * 4
+W3_AT = LANDED_AT + T
 
 
 def tile_list_linen_wear_pages_kernel(
@@ -53,21 +60,26 @@ def tile_list_linen_wear_pages_kernel(
         def half_list(tile, h):
             return tile[:, h * LIST_COLS : (h + 1) * LIST_COLS]
 
+        def bank(shape, tag):
+            return psum.tile(shape, F32, name="bank", tag=tag, bufs=BANKS[tag])
+
         def load_list(src, name):
             tile = lists.tile([P, S // 16], U16, name=name)
             nc.sync.dma_start(tile[:], src)
             return tile
 
-        def scale_tile(width, name, clear):
+        def zeroed_scales(width, name, engine):
             tile = keep.tile([P, width], U8, name=name, align_bytes=64)
-            clear.memset(tile[:].bitcast(I32), 0)
+            engine.memset(tile[:].bitcast(I32), 0)
             return tile
 
-        def load_scale_rows(tile, src, queue):
-            passes = src.shape[0]
-            for q in range(4):
-                queue.dma_start(
-                    tile[32 * q : 32 * q + 4 * passes, :].bitcast(I32),
+        def scale_rows(q, passes):
+            return slice(QUADRANT * q, QUADRANT * q + 4 * passes)
+
+        def load_scales(tile, src):
+            for q in range(P // QUADRANT):
+                nc.sync.dma_start(
+                    tile[scale_rows(q, src.shape[0]), :].bitcast(I32),
                     src[:, 4 * q : 4 * q + 4, :].bitcast(I32),
                 )
 
@@ -76,165 +88,166 @@ def tile_list_linen_wear_pages_kernel(
             nc.sync.dma_start(tile[:], tab_words[a].rearrange("p n t -> p (n t)").bitcast(I32))
             return tile
 
-        def load_weights(c):
-            cols = slice(c * P, (c + 1) * P)
+        def load_w1(c):
             raw = []
             for a in range(PASSES):
-                tile = keep.tile([P, 4, P], F32, name="w1_raw%d%d" % (c, a))
-                nc.sync.dma_start(
-                    tile[:], w1[512 * a : 512 * (a + 1), cols].rearrange("(p j) r -> p j r", j=4)
-                )
+                tile = keep.tile([P, PACK, P], F32, name="w1_raw%d%d" % (c, a))
+                rows = w1[K_PASS * a : K_PASS * (a + 1), c * P : (c + 1) * P]
+                nc.sync.dma_start(tile[:], rows.rearrange("(p t) r -> p t r", t=PACK))
                 raw.append(tile)
             return raw
 
         def load_w2(c):
-            cols = slice(c * P, (c + 1) * P)
-            w2c = keep.tile([P, PASSES, P], I32, name="w2_codes%d" % c, align_bytes=64)
-            nc.sync.dma_start(
-                w2c[:],
-                w2_words[:, :, cols, :].rearrange("a p n t -> p a (n t)").bitcast(I32),
-            )
-            return w2c
-
-        def load_rows(src, c, name):
-            tile = keep.tile([P, src.shape[1]], F32, name="%s%d" % (name, c))
-            nc.sync.dma_start(tile[:], src[c * P : (c + 1) * P, :])
-            return tile
-
-        def load_half(src, c, h, name):
-            label = "%s%d%d" % (name, c, h)
-            tile = keep.tile([P, HALF], F32, name=label, tag=label, align_bytes=64)
-            nc.sync.dma_start(tile[:], src[c * P : (c + 1) * P, half_cols(h)])
+            tile = keep.tile([P, PASSES, P], I32, name="w2_codes%d" % c, align_bytes=64)
+            codes = w2_words[:, :, c * P : (c + 1) * P, :].rearrange("a p n t -> p a (n t)")
+            nc.sync.dma_start(tile[:], codes.bitcast(I32))
             return tile
 
         def load_w3(part):
-            cols = slice(part * W3_PART, (part + 1) * W3_PART)
-            raw = shared.tile(
-                [P, 4, W3_PART], F32, name="w3_raw%d" % part, offset=PASSES * T * 4 + T + part * 16 * W3_PART
+            tile = shared.tile(
+                [P, PACK, W3_PART], F32, name="w3_raw%d" % part, offset=W3_AT + part * PACK * W3_PART * 4
             )
-            nc.sync.dma_start(raw[:], w3[:, cols].rearrange("(p j) n -> p j n", j=4))
-            return raw
+            cols = w3[:, part * W3_PART : (part + 1) * W3_PART]
+            nc.sync.dma_start(tile[:], cols.rearrange("(p t) n -> p t n", t=PACK))
+            return tile
+
+        def load_page0(c):
+            tile = keep.tile([P, T2], F32, name="page0_%d" % c)
+            nc.sync.dma_start(tile[:], page0[c * P : (c + 1) * P, :])
+            return tile
+
+        def load_unit(src, c, h, name):
+            tag = "%s%d%d" % (name, c, h)
+            tile = keep.tile([P, HALF], F32, name=tag, tag=tag, align_bytes=64)
+            nc.sync.dma_start(tile[:], src[c * P : (c + 1) * P, half_cols(h)])
+            return tile
 
         def interleave(dst, src):
             nc.scalar.copy(
-                dst.rearrange("p (c i t) -> p c t i", i=4, t=4),
-                src.rearrange("p t (c i) -> p c t i", i=4),
+                dst.rearrange("p (g i t) -> p g t i", i=4, t=PACK),
+                src.rearrange("p t (g i) -> p g t i", i=4),
             )
 
+        def quantise(grouped, codes, scales):
+            nc.vector.quantize_mx(codes[:].bitcast(FP8X4), scales[:], grouped)
+            return codes, scales
+
         idx = load_list(offs, "idx")
-        landed = shared.tile([P, T], U8, name="landed", offset=PASSES * T * 4)
-        load_scale_rows(landed, tab_scales, nc.sync)
-        tab_s = scale_tile(T, "tab_s", nc.vector)
-        for q in range(4):
-            rows = slice(32 * q, 32 * q + 4 * PASSES)
+        landed = shared.tile([P, T], U8, name="landed", offset=LANDED_AT)
+        load_scales(landed, tab_scales)
+        tab_s = zeroed_scales(T, "tab_s", nc.vector)
+        for q in range(P // QUADRANT):
+            rows = scale_rows(q, PASSES)
             nc.vector.tensor_copy(tab_s[rows, :].bitcast(I32), landed[rows, :].bitcast(I32))
-        w2_s = scale_tile(H, "w2_s", nc.gpsimd)
-        vectors = keep.tile([P, P], F32, name="vectors")
-        nc.gpsimd.memset(vectors[:], 0.0)
-        nc.gpsimd.dma_start(vectors[0:SLICES, :], gain.rearrange("(c p) -> c p", p=P))
-        nc.gpsimd.dma_start(vectors[SLICES : 2 * SLICES, :], lo.rearrange("(c p) -> c p", p=P))
+
+        def load_as_rows(vector, name, queue):
+            tile = keep.tile([P, P], F32, name=name + "_rows")
+            nc.gpsimd.memset(tile[:], 0.0)
+            queue.dma_start(tile[0:SLICES, :], vector.rearrange("(c p) -> c p", p=P))
+            return tile
+
+        def per_slice(as_rows, name):
+            flipped = bank([P, P], "turn")
+            nc.tensor.transpose(flipped[:], as_rows[:], ident[:])
+            tile = keep.tile([P, SLICES], F32, name=name)
+            nc.scalar.copy(tile[:], flipped[:, 0:SLICES])
+            return [tile[:, c : c + 1] for c in range(SLICES)]
+
+        gain_rows = load_as_rows(gain, "gain", nc.gpsimd)
+        w2_s = zeroed_scales(H, "w2_s", nc.gpsimd)
         ident = keep.tile([P, P], F32, name="ident")
         make_identity(nc, ident[:])
-        w4_s = scale_tile(N, "w4_s", nc.gpsimd)
-        turned_vectors = psum.tile([P, P], F32, name="turn_v", tag="turn", bufs=BANKS["turn"])
-        nc.tensor.transpose(turned_vectors[:], vectors[:], ident[:])
-        per_row = keep.tile([P, 2 * SLICES], F32, name="per_row")
-        nc.scalar.copy(per_row[:], turned_vectors[:, 0 : 2 * SLICES])
-        gain_c = per_row[:, 0:SLICES]
-        lo_c = per_row[:, SLICES : 2 * SLICES]
+        w4_s = zeroed_scales(N, "w4_s", nc.gpsimd)
+        gain_of = per_slice(gain_rows, "gain")
 
         words = [load_table_words(0)]
-        weights = [load_weights(0)]
-        w2_codes = [load_w2(0)]
-        load_scale_rows(w2_s, w2_scales, nc.sync)
+        w1_raw = [load_w1(0)]
+        load_scales(w2_s, w2_scales)
         words.append(load_table_words(1))
-        cycs = {(0, 0): load_half(cyc, 0, 0, "cyc")}
-        weights.append(load_weights(1))
-        cycs[0, 1] = load_half(cyc, 0, 1, "cyc")
-        wgs_sb = [load_half(wgs, 0, 0, "wgs")]
+        w2_codes = [load_w2(0)]
+        cyc_sb = {(0, 0): load_unit(cyc, 0, 0, "cyc")}
+        w1_raw.append(load_w1(1))
+        cyc_sb[0, 1] = load_unit(cyc, 0, 1, "cyc")
+        wgs_sb = [load_unit(wgs, 0, 0, "wgs")]
         idx2 = load_list(offs2, "idx2")
-        pages0 = [load_rows(page0, 0, "page0_")]
+        pages0 = [load_page0(0)]
         w2_codes.append(load_w2(1))
-        cycs[1, 0] = load_half(cyc, 1, 0, "cyc")
-        weights.append(load_weights(2))
+        cyc_sb[1, 0] = load_unit(cyc, 1, 0, "cyc")
+        w1_raw.append(load_w1(2))
         idx3 = load_list(offs3, "idx3")
-        wgs_sb.append(load_half(wgs, 0, 1, "wgs"))
-        cycs[1, 1] = load_half(cyc, 1, 1, "cyc")
-        weights.append(load_weights(3))
+        wgs_sb.append(load_unit(wgs, 0, 1, "wgs"))
+        cyc_sb[1, 1] = load_unit(cyc, 1, 1, "cyc")
+        w1_raw.append(load_w1(3))
         for c in range(1, SLICES):
-            pages0.append(load_rows(page0, c, "page0_"))
+            pages0.append(load_page0(c))
             if c + 1 < SLICES:
                 w2_codes.append(load_w2(c + 1))
                 for h in range(HALVES):
-                    cycs[c + 1, h] = load_half(cyc, c + 1, h, "cyc")
-        w3_raw = [load_w3(part) for part in range(SLICES - 1)]
+                    cyc_sb[c + 1, h] = load_unit(cyc, c + 1, h, "cyc")
+        lo_rows = load_as_rows(lo, "lo", nc.sync)
+        w3_raw = [load_w3(part) for part in range(W3_PARTS)]
 
-        v_codes = [[None] * HALVES for a in range(PASSES)]
         v_scales = keep.tile([P, S], U8, name="v_scales", align_bytes=64)
         nc.vector.tensor_copy(v_scales[:], tab_s[:].indirect(idx[:]))
+        v_codes = {}
         for a in range(PASSES):
             for h in range(HALVES):
-                picked = keep.tile([P, HALF], U32, name="v_codes%d%d" % (a, h), align_bytes=64)
-                nc.vector.tensor_copy(picked[:], words[a][:].bitcast(U32).indirect(half_list(idx, h)))
-                v_codes[a][h] = picked
+                v_codes[a, h] = keep.tile([P, HALF], U32, name="v_codes%d%d" % (a, h), align_bytes=64)
+                nc.vector.tensor_copy(v_codes[a, h][:], words[a][:].bitcast(U32).indirect(half_list(idx, h)))
 
         def quantise_w1(c):
-            raw = weights[c]
-            grouped = ring.tile([P, PASSES * 4 * P], BF16, name="w1_grouped", align_bytes=64)
+            grouped = ring.tile([P, PASSES * K_PASS], BF16, name="w1_grouped", align_bytes=64)
             for a in range(PASSES):
-                interleave(grouped[:, a * 4 * P : (a + 1) * 4 * P], raw[a][:])
-            codes = ring.tile([P, PASSES * P], U32, name="w1_codes", align_bytes=64, bufs=4)
-            scales = ring.tile([P, PASSES * P], U8, name="w1_scales", align_bytes=64, bufs=4)
-            nc.vector.quantize_mx(codes[:].bitcast(FP8X4), scales[:], grouped[:])
-            return codes, scales
+                interleave(grouped[:, a * K_PASS : (a + 1) * K_PASS], w1_raw[c][a][:])
+            codes = ring.tile([P, PASSES * P], U32, name="w1_codes", align_bytes=64, bufs=SLICES)
+            scales = ring.tile([P, PASSES * P], U8, name="w1_scales", align_bytes=64, bufs=SLICES)
+            return quantise(grouped[:], codes, scales)
 
         def turn_rows(values, turned, c, tag="turn"):
-            bank = psum.tile([P, 4, P], F32, name="turn_a", tag=tag, bufs=BANKS[tag])
-            for b in range(4):
-                nc.tensor.transpose(bank[:, b, :], values[:, b * P : (b + 1) * P], ident[:])
+            flipped = bank([P, HALF // P, P], tag)
+            for b in range(HALF // P):
+                nc.tensor.transpose(flipped[:, b, :], values[:, b * P : (b + 1) * P], ident[:])
+            mine = slice(c * P // PACK, (c + 1) * P // PACK)
             nc.scalar.copy(
-                turned[:].rearrange("j b (u p e) -> j b u p e", u=2, e=2)[:, :, :, 32 * c : 32 * (c + 1), :],
-                bank[:].rearrange("j b (q u e) -> j b u q e", u=2, e=2),
+                turned[:].rearrange("j b (u m e) -> j b u m e", u=2, e=2)[:, :, :, mine, :],
+                flipped[:].rearrange("j b (m u e) -> j b u m e", u=2, e=2),
             )
 
-        def turn_back(turned, name, tag="turn"):
+        def turn_back(turned, tag):
             pairs = turned[:].rearrange("j b w -> j (b w)").bitcast(F32)
-            grouped = keep.tile([P, 4 * HALF], BF16, name=name + "_grouped", tag=name + "_grouped", align_bytes=64)
+            grouped = keep.tile([P, PACK * HALF], BF16, name="grouped", tag=tag, align_bytes=64)
             for g in range(2):
-                bank = psum.tile([P, 2, 2, P], F32, name="turn_b", tag=tag, bufs=BANKS[tag])
+                flipped = bank([P, 2, 2, P], "turn")
                 for b in range(2):
                     for u in range(2):
                         first = (2 * (2 * g + b) + u) * P
-                        nc.tensor.transpose(bank[:, b, u, :], pairs[:, first : first + P], ident[:])
+                        nc.tensor.transpose(flipped[:, b, u, :], pairs[:, first : first + P], ident[:])
                 nc.scalar.copy(
-                    grouped[:].bitcast(F32)[:, g * 4 * P : (g + 1) * 4 * P].rearrange(
-                        "p (b j u) -> p b j u", b=2, u=2
-                    ),
-                    bank[:].rearrange("p b u j -> p b j u"),
+                    grouped[:].bitcast(F32)[:, half_cols(g)].rearrange("p (b j u) -> p b j u", b=2, u=2),
+                    flipped[:].rearrange("p b u j -> p b j u"),
                 )
             return grouped
 
         def quantise_half(grouped, name, tag):
             codes = keep.tile([P, HALF], U32, name=name + "_codes", tag=tag, align_bytes=64)
             scales = keep.tile([P, HALF], U8, name=name + "_scales", align_bytes=64)
-            nc.vector.quantize_mx(codes[:].bitcast(FP8X4), scales[:], grouped[:])
-            return codes, scales
+            return quantise(grouped[:], codes, scales)
 
-        h_turned = [keep.tile([P, 4, H], BF16, name="h_turned%d" % h, tag="turned%d" % h) for h in range(HALVES)]
+        h_turned = [
+            keep.tile([P, HALF // P, H], BF16, name="h_turned%d" % h, tag="turned%d" % h) for h in range(HALVES)
+        ]
         w1_q = [quantise_w1(0)]
 
         def state(c, h):
             w1_codes, w1_scales = w1_q[c]
-            w2c = w2_codes[c]
-            cols = slice(c * P, (c + 1) * P)
-            sum_a = psum.tile([P, HALF], F32, name="sum_a", tag="sum_a")
-            sum_b = psum.tile([P, HALF], F32, name="sum_b", tag="sum_b")
+            sum_a = bank([P, HALF], "sum_a")
+            sum_b = bank([P, HALF], "sum_b")
             for a in range(PASSES):
                 nc.tensor.matmul_mx(
                     sum_a[:],
                     lhsT=w1_codes[:, a * P : (a + 1) * P].bitcast(FP8X4),
                     lhsT_scale=w1_scales[:, a * P : (a + 1) * P],
-                    rhs=v_codes[a][h][:].bitcast(FP8X4),
+                    rhs=v_codes[a, h][:].bitcast(FP8X4),
                     rhs_scale=v_scales[4 * a :, half_cols(h)],
                     start=(a == 0),
                     stop=(a == PASSES - 1),
@@ -242,115 +255,119 @@ def tile_list_linen_wear_pages_kernel(
             for a in range(PASSES):
                 nc.tensor.matmul_mx(
                     sum_b[:],
-                    lhsT=w2c[:, a, :].bitcast(FP8X4),
-                    lhsT_scale=w2_s[4 * a :, cols],
-                    rhs=v_codes[a][h][:].bitcast(FP8X4),
+                    lhsT=w2_codes[c][:, a, :].bitcast(FP8X4),
+                    lhsT_scale=w2_s[4 * a :, c * P : (c + 1) * P],
+                    rhs=v_codes[a, h][:].bitcast(FP8X4),
                     rhs_scale=v_scales[4 * a :, half_cols(h)],
                     start=(a == 0),
                     stop=(a == PASSES - 1),
                 )
-            squashed = ring.tile([P, HALF], F32, name="squashed", tag="ring_a", bufs=7)
+            squashed = ring.tile([P, HALF], F32, name="squashed", tag="from_psum", bufs=FROM_PSUM_BUFS)
             nc.scalar.activation(squashed[:], sum_a[:], TANH)
-            u = units.index((c, h))
-            prod = squashed if u < VECTOR_SUMS else product
-            factors = cycs[c, h][:]
-            if (c, h) == units[0]:
-                nc.vector.scalar_tensor_tensor(prod[:], squashed[:], gain_c[:, c : c + 1], factors, MULT, MULT)
+            product = squashed if c == 0 else shared_product
+            factors = cyc_sb[c, h][:]
+            if (c, h) == (0, 0):
+                nc.vector.scalar_tensor_tensor(product[:], squashed[:], gain_of[c], factors, MULT, MULT)
             else:
-                nc.scalar.activation(factors, factors, COPY, scale=gain_c[:, c : c + 1])
-                nc.gpsimd.tensor_tensor(prod[:], squashed[:], factors, MULT)
-            new = ring.tile([P, HALF], F32, name="new", tag="new", bufs=7)
-            if u < VECTOR_SUMS:
-                nc.vector.scalar_tensor_tensor(new[:], sum_b[:], gain_c[:, c : c + 1], prod[:], MULT, ADD)
+                nc.scalar.activation(factors, factors, COPY, scale=gain_of[c])
+                nc.gpsimd.tensor_tensor(product[:], squashed[:], factors, MULT)
+            if h == 0 and 0 < c < SLICES - 1:
+                new = keep.tile([P, HALF], F32, name="new", tag="state%d" % c, align_bytes=64)
             else:
-                nc.scalar.activation(new[:], sum_b[:], COPY, scale=gain_c[:, c : c + 1])
-                nc.gpsimd.tensor_tensor(new[:], new[:], prod[:], ADD)
+                new = ring.tile([P, HALF], F32, name="new", tag="values", bufs=STATE_BUFS)
+            if c == 0:
+                nc.vector.scalar_tensor_tensor(new[:], sum_b[:], gain_of[c], product[:], MULT, ADD)
+            else:
+                nc.scalar.activation(new[:], sum_b[:], COPY, scale=gain_of[c])
+                nc.gpsimd.tensor_tensor(new[:], new[:], product[:], ADD)
             return new
 
         def put(c, h, new):
-            u = units.index((c, h))
-            if u == len(units) - 1:
-                placed = keep.tile([P, HALF], F32, name="placed_last", tag="late")
+            window = pages0[c][:].indirect(half_list(idx2, h))
+            if (c, h) == (SLICES - 1, HALVES - 1):
+                nc.vector.tensor_tensor(window, new[:], wgs_sb[h][:], MULT)
             else:
-                placed = cycs[c, h]
-            engine = nc.vector if u < VECTOR_SUMS else nc.gpsimd
-            engine.tensor_tensor(placed[:], new[:], wgs_sb[h][:], MULT)
-            nc.vector.tensor_copy(pages0[c][:].indirect(half_list(idx2, h)), placed[:])
-            if u < VECTOR_SUMS:
-                waiting.append((new, c, h))
-            else:
-                turn_rows(new[:], h_turned[h], c)
-            if u == LATE_TURN:
-                for state_tile, its_c, its_h in waiting:
-                    turn_rows(state_tile[:], h_turned[its_h], its_c)
+                engine = nc.vector if c == 0 else nc.gpsimd
+                engine.tensor_tensor(cyc_sb[c, h][:], new[:], wgs_sb[h][:], MULT)
+                nc.vector.tensor_copy(window, cyc_sb[c, h][:])
 
-        units = [(c, h) for c in range(SLICES) for h in range(HALVES)]
-        waiting = []
-        product = keep.tile([P, HALF], F32, name="product", tag="product")
-        for c, h in units:
-            put(c, h, state(c, h))
-            if len(w1_q) < SLICES:
-                w1_q.append(quantise_w1(len(w1_q)))
-        w3_grouped = keep.tile([P, 4 * N], BF16, name="w3_grouped", align_bytes=64)
-        for part in range(SLICES - 1):
-            interleave(w3_grouped[:, 4 * part * W3_PART : 4 * (part + 1) * W3_PART], w3_raw[part][:])
+        shared_product = keep.tile([P, HALF], F32, name="shared_product", tag="product")
+        first_slice = []
+        for c in range(SLICES):
+            for h in range(HALVES):
+                new = state(c, h)
+                put(c, h, new)
+                if c == 0:
+                    first_slice.append(new)
+                else:
+                    turn_rows(new[:], h_turned[h], c)
+                if (c, h) == (SLICES - 2, HALVES - 1):
+                    for its_h, its_state in enumerate(first_slice):
+                        turn_rows(its_state[:], h_turned[its_h], 0)
+                    lo_of = per_slice(lo_rows, "lo")
+                if (c, h) == (SLICES - 1, 0):
+                    h0_grouped = turn_back(h_turned[0], "grouped_a")
+                if len(w1_q) < SLICES:
+                    w1_q.append(quantise_w1(len(w1_q)))
+        w3_grouped = keep.tile([P, PACK * N], BF16, name="w3_grouped", align_bytes=64)
+        for part in range(W3_PARTS):
+            interleave(w3_grouped[:, PACK * part * W3_PART : PACK * (part + 1) * W3_PART], w3_raw[part][:])
 
         w4_codes = keep.tile([P, 2 * N], U8, name="w4_codes", align_bytes=64)
         nc.sync.dma_start(w4_codes[:].bitcast(I32), w4_words[0].bitcast(I32))
-        load_scale_rows(w4_s, w4_scales, nc.sync)
+        load_scales(w4_s, w4_scales)
         idx4 = load_list(offs4, "idx4")
         wgo_sb = keep.tile([P, S], F32, name="wgo_sb")
         nc.sync.dma_start(wgo_sb[:], wgo)
-        pages = []
+        pages1 = []
         for nb in range(BLOCKS):
             page = shared.tile([P, T2], F32, name="page1_%d" % nb, offset=nb * T2 * 4)
             nc.sync.dma_start(page[:], page1[nb * P : (nb + 1) * P, :])
-            pages.append(page)
+            pages1.append(page)
 
-        h_q = [quantise_half(turn_back(h_turned[0], "h0"), "h0", "wgs01")]
+        h_q = [quantise_half(h0_grouped, "h0", "cyc%d%d" % (SLICES - 1, HALVES - 1))]
 
         def recall(c, h, fetched, floored):
             nc.vector.tensor_copy(fetched, pages0[c][:].indirect(half_list(idx3, h)))
-            nc.gpsimd.tensor_scalar(floored, fetched, F32_MAX, lo_c[:, c : c + 1], MIN, MAX)
+            nc.gpsimd.tensor_scalar(floored, fetched, F32_MAX, lo_of[c], MIN, MAX)
 
         def quantise_w3(first, last, tag):
             codes = keep.tile([P, last - first], U32, name="w3_codes", tag=tag, align_bytes=64)
             scales = keep.tile([P, last - first], U8, name="w3_scales%d" % first, align_bytes=64)
-            nc.vector.quantize_mx(codes[:].bitcast(FP8X4), scales[:], w3_grouped[:, 4 * first : 4 * last])
+            quantise(w3_grouped[:, PACK * first : PACK * last], codes, scales)
             return [(codes[:, n : n + P], scales[:, n : n + P]) for n in range(0, last - first, P)]
 
-        x_turned = keep.tile([P, 4, H], BF16, name="x_turned0")
-        floored = keep.tile([P, SLICES, HALF], F32, name="floored", tag="product")
-        for c, tag in enumerate(("cyc00", "cyc01", "cyc10", "w3_codes")):
+        x0_turned = keep.tile([P, HALF // P, H], BF16, name="x0_turned")
+        x0 = keep.tile([P, SLICES, HALF], F32, name="x0", tag="product")
+        for c, tag in enumerate(("state1", "state2", "cyc10", "w3_codes")):
             fetched = keep.tile([P, HALF], F32, name="fetched", tag=tag, align_bytes=64)
-            recall(c, 0, fetched[:], floored[:, c, :])
-            turn_rows(floored[:, c, :], x_turned, c)
-        x_grouped = turn_back(x_turned, "x0")
-        late = keep.tile([P, SLICES, HALF], F32, name="late", tag="late")
+            recall(c, 0, fetched[:], x0[:, c, :])
+            turn_rows(x0[:, c, :], x0_turned, c)
+        x0_grouped = turn_back(x0_turned, "grouped_b")
+        x1 = keep.tile([P, SLICES, HALF], F32, name="x1", tag="wgs01", align_bytes=64)
         for c in range(SLICES):
-            recall(c, 1, late[:, c, :], late[:, c, :])
+            recall(c, 1, x1[:, c, :], x1[:, c, :])
         w3_q = quantise_w3(0, HALF, "w3_codes")
-        x_q = [quantise_half(x_grouped, "x0", "x0_codes")]
-        w3_q.extend(quantise_w3(HALF, N, "x0_grouped"))
+        x_q = [quantise_half(x0_grouped, "x0", "x0_codes")]
+        w3_q.extend(quantise_w3(HALF, N, "grouped_b"))
 
         def fresh(nb, h, tag="turn"):
-            cols = slice(nb * P, (nb + 1) * P)
-            sum_2 = psum.tile([P, HALF], F32, name="sum_2", tag=tag, bufs=BANKS[tag])
+            sum_2 = bank([P, HALF], tag)
             nc.tensor.matmul_mx(
                 sum_2[:],
                 lhsT=w4_codes[:, 2 * nb * P : 2 * (nb + 1) * P].bitcast(FP4X4),
-                lhsT_scale=w4_s[:, cols],
+                lhsT_scale=w4_s[:, nb * P : (nb + 1) * P],
                 rhs=h_q[h][0][:].bitcast(FP8X4),
                 rhs_scale=h_q[h][1][:],
                 start=True,
                 stop=True,
             )
-            y2 = ring.tile([P, HALF], F32, name="y2", tag="ring_a", bufs=7)
+            y2 = ring.tile([P, HALF], F32, name="y2", tag="from_psum", bufs=FROM_PSUM_BUFS)
             nc.scalar.copy(y2[:], sum_2[:])
             return y2
 
         def place(nb, h, y2, tag="sum_a", y=None):
-            sum_1 = psum.tile([P, HALF], F32, name="sum_1", tag=tag)
+            sum_1 = bank([P, HALF], tag)
             nc.tensor.matmul_mx(
                 sum_1[:],
                 lhsT=w3_q[nb][0].bitcast(FP8X4),
@@ -361,28 +378,27 @@ def tile_list_linen_wear_pages_kernel(
                 stop=True,
             )
             if y is None:
-                y = ring.tile([P, HALF], F32, name="y", tag="new", bufs=7)
+                y = ring.tile([P, HALF], F32, name="y", tag="values", bufs=STATE_BUFS)
             nc.vector.tensor_tensor(y[:], sum_1[:], y2[:], MAX)
-            nc.vector.tensor_tensor(
-                pages[nb][:].indirect(half_list(idx4, h)), y[:], wgo_sb[:, half_cols(h)], MULT
-            )
+            window = pages1[nb][:].indirect(half_list(idx4, h))
+            nc.vector.tensor_tensor(window, y[:], wgo_sb[:, half_cols(h)], MULT)
 
         place(0, 0, fresh(0, 0))
         place(1, 0, fresh(1, 0))
-        early = [fresh(nb, 0, "sum_a") for nb in (2, 3, 4)]
-        x_turned = keep.tile([P, 4, H], BF16, name="x_turned1", tag="turned0")
+        y2_of = {nb: fresh(nb, 0, "sum_a") for nb in range(2, BLOCKS - 1)}
+        x1_turned = keep.tile([P, HALF // P, H], BF16, name="x1_turned", tag="turned0")
         for c in range(SLICES):
-            turn_rows(late[:, c, :], x_turned, c, "sum_a")
-        x_grouped = turn_back(x_turned, "h0")
-        h_grouped = turn_back(h_turned[1], "h1")
-        place(2, 0, early[0], "sum_b")
-        x_q.append(quantise_half(x_grouped, "x1", "x1_codes"))
-        h_q.append(quantise_half(h_grouped, "h1", "h1_codes"))
-        held = keep.tile([P, HALF], F32, name="held_y", tag="h1_grouped", align_bytes=64)
-        place(3, 0, early[1], "sum_b", held)
-        place(4, 0, early[2])
+            turn_rows(x1[:, c, :], x1_turned, c, "sum_a")
+        x1_grouped = turn_back(x1_turned, "grouped_a")
+        h1_grouped = turn_back(h_turned[1], "grouped_c")
+        place(2, 0, y2_of[2], "sum_b")
+        x_q.append(quantise_half(x1_grouped, "x1", "x1_codes"))
+        h_q.append(quantise_half(h1_grouped, "h1", "h1_codes"))
+        behind = keep.tile([P, HALF], F32, name="behind", tag="grouped_c", align_bytes=64)
+        place(3, 0, y2_of[3], "sum_b", behind)
+        place(4, 0, y2_of[4])
         for nb in range(BLOCKS):
             place(nb, 1, fresh(nb, 1))
-            nc.sync.dma_start(out[nb * P : (nb + 1) * P, :], pages[nb][:])
+            nc.sync.dma_start(out[nb * P : (nb + 1) * P, :], pages1[nb][:])
             if nb == 0:
-                place(5, 0, fresh(5, 0))
+                place(BLOCKS - 1, 0, fresh(BLOCKS - 1, 0))

from contextlib import ExitStack

import concourse.mybir as mybir
from concourse.masks import make_identity

K, H, N, T, S, T2 = 1024, 512, 768, 4096, 1024, 2048
FLOPS = 2 * S * (2 * K * H + 2 * H * N)

F32 = mybir.dt.float32
BF16 = mybir.dt.bfloat16
I32 = mybir.dt.int32
U32 = mybir.dt.uint32
U16 = mybir.dt.uint16
U8 = mybir.dt.uint8
FP8X4 = mybir.dt.float8_e4m3fn_x4
FP4X4 = mybir.dt.float4_e2m1fn_x4
MULT = mybir.AluOpType.mult
ADD = mybir.AluOpType.add
MAX = mybir.AluOpType.max
MIN = mybir.AluOpType.min
TANH = mybir.ActivationFunctionType.Tanh
COPY = mybir.ActivationFunctionType.Copy
F32_MAX = 3.4028234663852886e38

P = 128
PACK = 4
K_PASS = P * PACK
PASSES = K // K_PASS
QUADRANT = 32
SLICES = H // P
BLOCKS = N // P
HALF = 512
HALVES = S // HALF
LIST_COLS = HALF // 16
W3_PARTS = 3
W3_PART = N // W3_PARTS
BANKS = {"turn": 4, "sum_a": 2, "sum_b": 2}
FROM_PSUM_BUFS = 7
STATE_BUFS = 6

LANDED_AT = PASSES * T * 4
W3_AT = LANDED_AT + T


def tile_list_linen_wear_pages_kernel(
    tc, tab_words, tab_scales, offs, offs2, offs3, offs4, w1, w2_words, w2_scales, cyc, gain, wgs,
    page0, lo, w3, w4_words, w4_scales, wgo, page1, out,
):
    nc = tc.nc
    with ExitStack() as ctx:
        lists = ctx.enter_context(tc.tile_pool(name="lists", bufs=1))
        keep = ctx.enter_context(tc.tile_pool(name="keep", bufs=1))
        shared = ctx.enter_context(tc.tile_pool(name="shared", bufs=1))
        ring = ctx.enter_context(tc.tile_pool(name="ring", bufs=2))
        psum = ctx.enter_context(tc.psum_pool(name="psum", bufs=2))

        def half_cols(h):
            return slice(h * HALF, (h + 1) * HALF)

        def half_list(tile, h):
            return tile[:, h * LIST_COLS : (h + 1) * LIST_COLS]

        def bank(shape, tag):
            return psum.tile(shape, F32, name="bank", tag=tag, bufs=BANKS[tag])

        def load_list(src, name):
            tile = lists.tile([P, S // 16], U16, name=name)
            nc.sync.dma_start(tile[:], src)
            return tile

        def zeroed_scales(width, name, engine):
            tile = keep.tile([P, width], U8, name=name, align_bytes=64)
            engine.memset(tile[:].bitcast(I32), 0)
            return tile

        def scale_rows(q, passes):
            return slice(QUADRANT * q, QUADRANT * q + 4 * passes)

        def load_scales(tile, src):
            for q in range(P // QUADRANT):
                nc.sync.dma_start(
                    tile[scale_rows(q, src.shape[0]), :].bitcast(I32),
                    src[:, 4 * q : 4 * q + 4, :].bitcast(I32),
                )

        def load_table_words(a):
            tile = shared.tile([P, T], I32, name="tab_words%d" % a, offset=a * T * 4)
            nc.sync.dma_start(tile[:], tab_words[a].rearrange("p n t -> p (n t)").bitcast(I32))
            return tile

        def load_w1(c):
            raw = []
            for a in range(PASSES):
                tile = keep.tile([P, PACK, P], F32, name="w1_raw%d%d" % (c, a))
                rows = w1[K_PASS * a : K_PASS * (a + 1), c * P : (c + 1) * P]
                nc.sync.dma_start(tile[:], rows.rearrange("(p t) r -> p t r", t=PACK))
                raw.append(tile)
            return raw

        def load_w2(c):
            tile = keep.tile([P, PASSES, P], I32, name="w2_codes%d" % c, align_bytes=64)
            codes = w2_words[:, :, c * P : (c + 1) * P, :].rearrange("a p n t -> p a (n t)")
            nc.sync.dma_start(tile[:], codes.bitcast(I32))
            return tile

        def load_w3(part):
            tile = shared.tile(
                [P, PACK, W3_PART], F32, name="w3_raw%d" % part, offset=W3_AT + part * PACK * W3_PART * 4
            )
            cols = w3[:, part * W3_PART : (part + 1) * W3_PART]
            nc.sync.dma_start(tile[:], cols.rearrange("(p t) n -> p t n", t=PACK))
            return tile

        def load_page0(c):
            tile = keep.tile([P, T2], F32, name="page0_%d" % c)
            nc.sync.dma_start(tile[:], page0[c * P : (c + 1) * P, :])
            return tile

        def load_unit(src, c, h, name):
            tag = "%s%d%d" % (name, c, h)
            tile = keep.tile([P, HALF], F32, name=tag, tag=tag, align_bytes=64)
            nc.sync.dma_start(tile[:], src[c * P : (c + 1) * P, half_cols(h)])
            return tile

        def interleave(dst, src):
            nc.scalar.copy(
                dst.rearrange("p (g i t) -> p g t i", i=4, t=PACK),
                src.rearrange("p t (g i) -> p g t i", i=4),
            )

        def quantise(grouped, codes, scales):
            nc.vector.quantize_mx(codes[:].bitcast(FP8X4), scales[:], grouped)
            return codes, scales

        idx = load_list(offs, "idx")
        landed = shared.tile([P, T], U8, name="landed", offset=LANDED_AT)
        load_scales(landed, tab_scales)
        tab_s = zeroed_scales(T, "tab_s", nc.vector)
        for q in range(P // QUADRANT):
            rows = scale_rows(q, PASSES)
            nc.vector.tensor_copy(tab_s[rows, :].bitcast(I32), landed[rows, :].bitcast(I32))

        def load_as_rows(vector, name, queue):
            tile = keep.tile([P, P], F32, name=name + "_rows")
            nc.gpsimd.memset(tile[:], 0.0)
            queue.dma_start(tile[0:SLICES, :], vector.rearrange("(c p) -> c p", p=P))
            return tile

        def per_slice(as_rows, name):
            flipped = bank([P, P], "turn")
            nc.tensor.transpose(flipped[:], as_rows[:], ident[:])
            tile = keep.tile([P, SLICES], F32, name=name)
            nc.scalar.copy(tile[:], flipped[:, 0:SLICES])
            return [tile[:, c : c + 1] for c in range(SLICES)]

        gain_rows = load_as_rows(gain, "gain", nc.gpsimd)
        w2_s = zeroed_scales(H, "w2_s", nc.gpsimd)
        ident = keep.tile([P, P], F32, name="ident")
        make_identity(nc, ident[:])
        w4_s = zeroed_scales(N, "w4_s", nc.gpsimd)
        gain_of = per_slice(gain_rows, "gain")

        words = [load_table_words(0)]
        w1_raw = [load_w1(0)]
        load_scales(w2_s, w2_scales)
        words.append(load_table_words(1))
        w2_codes = [load_w2(0)]
        cyc_sb = {(0, 0): load_unit(cyc, 0, 0, "cyc")}
        w1_raw.append(load_w1(1))
        cyc_sb[0, 1] = load_unit(cyc, 0, 1, "cyc")
        wgs_sb = [load_unit(wgs, 0, 0, "wgs")]
        idx2 = load_list(offs2, "idx2")
        pages0 = [load_page0(0)]
        w2_codes.append(load_w2(1))
        cyc_sb[1, 0] = load_unit(cyc, 1, 0, "cyc")
        w1_raw.append(load_w1(2))
        idx3 = load_list(offs3, "idx3")
        wgs_sb.append(load_unit(wgs, 0, 1, "wgs"))
        cyc_sb[1, 1] = load_unit(cyc, 1, 1, "cyc")
        w1_raw.append(load_w1(3))
        for c in range(1, SLICES):
            pages0.append(load_page0(c))
            if c + 1 < SLICES:
                w2_codes.append(load_w2(c + 1))
                for h in range(HALVES):
                    cyc_sb[c + 1, h] = load_unit(cyc, c + 1, h, "cyc")
        lo_rows = load_as_rows(lo, "lo", nc.sync)
        w3_raw = [load_w3(part) for part in range(W3_PARTS)]

        v_scales = keep.tile([P, S], U8, name="v_scales", align_bytes=64)
        nc.vector.tensor_copy(v_scales[:], tab_s[:].indirect(idx[:]))
        v_codes = {}
        for a in range(PASSES):
            for h in range(HALVES):
                v_codes[a, h] = keep.tile([P, HALF], U32, name="v_codes%d%d" % (a, h), align_bytes=64)
                nc.vector.tensor_copy(v_codes[a, h][:], words[a][:].bitcast(U32).indirect(half_list(idx, h)))

        def quantise_w1(c):
            grouped = ring.tile([P, PASSES * K_PASS], BF16, name="w1_grouped", align_bytes=64)
            for a in range(PASSES):
                interleave(grouped[:, a * K_PASS : (a + 1) * K_PASS], w1_raw[c][a][:])
            codes = ring.tile([P, PASSES * P], U32, name="w1_codes", align_bytes=64, bufs=SLICES)
            scales = ring.tile([P, PASSES * P], U8, name="w1_scales", align_bytes=64, bufs=SLICES)
            return quantise(grouped[:], codes, scales)

        def turn_rows(values, turned, c, tag="turn"):
            flipped = bank([P, HALF // P, P], tag)
            for b in range(HALF // P):
                nc.tensor.transpose(flipped[:, b, :], values[:, b * P : (b + 1) * P], ident[:])
            mine = slice(c * P // PACK, (c + 1) * P // PACK)
            nc.scalar.copy(
                turned[:].rearrange("j b (u m e) -> j b u m e", u=2, e=2)[:, :, :, mine, :],
                flipped[:].rearrange("j b (m u e) -> j b u m e", u=2, e=2),
            )

        def turn_back(turned, tag):
            pairs = turned[:].rearrange("j b w -> j (b w)").bitcast(F32)
            grouped = keep.tile([P, PACK * HALF], BF16, name="grouped", tag=tag, align_bytes=64)
            for g in range(2):
                flipped = bank([P, 2, 2, P], "turn")
                for b in range(2):
                    for u in range(2):
                        first = (2 * (2 * g + b) + u) * P
                        nc.tensor.transpose(flipped[:, b, u, :], pairs[:, first : first + P], ident[:])
                nc.scalar.copy(
                    grouped[:].bitcast(F32)[:, half_cols(g)].rearrange("p (b j u) -> p b j u", b=2, u=2),
                    flipped[:].rearrange("p b u j -> p b j u"),
                )
            return grouped

        def quantise_half(grouped, name, tag):
            codes = keep.tile([P, HALF], U32, name=name + "_codes", tag=tag, align_bytes=64)
            scales = keep.tile([P, HALF], U8, name=name + "_scales", align_bytes=64)
            return quantise(grouped[:], codes, scales)

        h_turned = [
            keep.tile([P, HALF // P, H], BF16, name="h_turned%d" % h, tag="turned%d" % h) for h in range(HALVES)
        ]
        w1_q = [quantise_w1(0)]

        def state(c, h):
            w1_codes, w1_scales = w1_q[c]
            sum_a = bank([P, HALF], "sum_a")
            sum_b = bank([P, HALF], "sum_b")
            for a in range(PASSES):
                nc.tensor.matmul_mx(
                    sum_a[:],
                    lhsT=w1_codes[:, a * P : (a + 1) * P].bitcast(FP8X4),
                    lhsT_scale=w1_scales[:, a * P : (a + 1) * P],
                    rhs=v_codes[a, h][:].bitcast(FP8X4),
                    rhs_scale=v_scales[4 * a :, half_cols(h)],
                    start=(a == 0),
                    stop=(a == PASSES - 1),
                )
            for a in range(PASSES):
                nc.tensor.matmul_mx(
                    sum_b[:],
                    lhsT=w2_codes[c][:, a, :].bitcast(FP8X4),
                    lhsT_scale=w2_s[4 * a :, c * P : (c + 1) * P],
                    rhs=v_codes[a, h][:].bitcast(FP8X4),
                    rhs_scale=v_scales[4 * a :, half_cols(h)],
                    start=(a == 0),
                    stop=(a == PASSES - 1),
                )
            squashed = ring.tile([P, HALF], F32, name="squashed", tag="from_psum", bufs=FROM_PSUM_BUFS)
            nc.scalar.activation(squashed[:], sum_a[:], TANH)
            product = squashed if c == 0 else shared_product
            factors = cyc_sb[c, h][:]
            if (c, h) == (0, 0):
                nc.vector.scalar_tensor_tensor(product[:], squashed[:], gain_of[c], factors, MULT, MULT)
            else:
                nc.scalar.activation(factors, factors, COPY, scale=gain_of[c])
                nc.gpsimd.tensor_tensor(product[:], squashed[:], factors, MULT)
            if h == 0 and 0 < c < SLICES - 1:
                new = keep.tile([P, HALF], F32, name="new", tag="state%d" % c, align_bytes=64)
            else:
                new = ring.tile([P, HALF], F32, name="new", tag="values", bufs=STATE_BUFS)
            if c == 0:
                nc.vector.scalar_tensor_tensor(new[:], sum_b[:], gain_of[c], product[:], MULT, ADD)
            else:
                nc.scalar.activation(new[:], sum_b[:], COPY, scale=gain_of[c])
                nc.gpsimd.tensor_tensor(new[:], new[:], product[:], ADD)
            return new

        def put(c, h, new):
            window = pages0[c][:].indirect(half_list(idx2, h))
            if (c, h) == (SLICES - 1, HALVES - 1):
                nc.vector.tensor_tensor(window, new[:], wgs_sb[h][:], MULT)
            else:
                engine = nc.vector if c == 0 else nc.gpsimd
                engine.tensor_tensor(cyc_sb[c, h][:], new[:], wgs_sb[h][:], MULT)
                nc.vector.tensor_copy(window, cyc_sb[c, h][:])

        shared_product = keep.tile([P, HALF], F32, name="shared_product", tag="product")
        first_slice = []
        for c in range(SLICES):
            for h in range(HALVES):
                new = state(c, h)
                put(c, h, new)
                if c == 0:
                    first_slice.append(new)
                else:
                    turn_rows(new[:], h_turned[h], c)
                if (c, h) == (SLICES - 2, HALVES - 1):
                    for its_h, its_state in enumerate(first_slice):
                        turn_rows(its_state[:], h_turned[its_h], 0)
                    lo_of = per_slice(lo_rows, "lo")
                if (c, h) == (SLICES - 1, 0):
                    h0_grouped = turn_back(h_turned[0], "grouped_a")
                if len(w1_q) < SLICES:
                    w1_q.append(quantise_w1(len(w1_q)))
        w3_grouped = keep.tile([P, PACK * N], BF16, name="w3_grouped", align_bytes=64)
        for part in range(W3_PARTS):
            interleave(w3_grouped[:, PACK * part * W3_PART : PACK * (part + 1) * W3_PART], w3_raw[part][:])

        w4_codes = keep.tile([P, 2 * N], U8, name="w4_codes", align_bytes=64)
        nc.sync.dma_start(w4_codes[:].bitcast(I32), w4_words[0].bitcast(I32))
        load_scales(w4_s, w4_scales)
        idx4 = load_list(offs4, "idx4")
        wgo_sb = keep.tile([P, S], F32, name="wgo_sb")
        nc.sync.dma_start(wgo_sb[:], wgo)
        pages1 = []
        for nb in range(BLOCKS):
            page = shared.tile([P, T2], F32, name="page1_%d" % nb, offset=nb * T2 * 4)
            nc.sync.dma_start(page[:], page1[nb * P : (nb + 1) * P, :])
            pages1.append(page)

        h_q = [quantise_half(h0_grouped, "h0", "cyc%d%d" % (SLICES - 1, HALVES - 1))]

        def recall(c, h, fetched, floored):
            nc.vector.tensor_copy(fetched, pages0[c][:].indirect(half_list(idx3, h)))
            nc.gpsimd.tensor_scalar(floored, fetched, F32_MAX, lo_of[c], MIN, MAX)

        def quantise_w3(first, last, tag):
            codes = keep.tile([P, last - first], U32, name="w3_codes", tag=tag, align_bytes=64)
            scales = keep.tile([P, last - first], U8, name="w3_scales%d" % first, align_bytes=64)
            quantise(w3_grouped[:, PACK * first : PACK * last], codes, scales)
            return [(codes[:, n : n + P], scales[:, n : n + P]) for n in range(0, last - first, P)]

        x0_turned = keep.tile([P, HALF // P, H], BF16, name="x0_turned")
        x0 = keep.tile([P, SLICES, HALF], F32, name="x0", tag="product")
        for c, tag in enumerate(("state1", "state2", "cyc10", "w3_codes")):
            fetched = keep.tile([P, HALF], F32, name="fetched", tag=tag, align_bytes=64)
            recall(c, 0, fetched[:], x0[:, c, :])
            turn_rows(x0[:, c, :], x0_turned, c)
        x0_grouped = turn_back(x0_turned, "grouped_b")
        x1 = keep.tile([P, SLICES, HALF], F32, name="x1", tag="wgs01", align_bytes=64)
        for c in range(SLICES):
            recall(c, 1, x1[:, c, :], x1[:, c, :])
        w3_q = quantise_w3(0, HALF, "w3_codes")
        x_q = [quantise_half(x0_grouped, "x0", "x0_codes")]
        w3_q.extend(quantise_w3(HALF, N, "grouped_b"))

        def fresh(nb, h, tag="turn"):
            sum_2 = bank([P, HALF], tag)
            nc.tensor.matmul_mx(
                sum_2[:],
                lhsT=w4_codes[:, 2 * nb * P : 2 * (nb + 1) * P].bitcast(FP4X4),
                lhsT_scale=w4_s[:, nb * P : (nb + 1) * P],
                rhs=h_q[h][0][:].bitcast(FP8X4),
                rhs_scale=h_q[h][1][:],
                start=True,
                stop=True,
            )
            y2 = ring.tile([P, HALF], F32, name="y2", tag="from_psum", bufs=FROM_PSUM_BUFS)
            nc.scalar.copy(y2[:], sum_2[:])
            return y2

        def place(nb, h, y2, tag="sum_a", y=None):
            sum_1 = bank([P, HALF], tag)
            nc.tensor.matmul_mx(
                sum_1[:],
                lhsT=w3_q[nb][0].bitcast(FP8X4),
                lhsT_scale=w3_q[nb][1],
                rhs=x_q[h][0][:].bitcast(FP8X4),
                rhs_scale=x_q[h][1][:],
                start=True,
                stop=True,
            )
            if y is None:
                y = ring.tile([P, HALF], F32, name="y", tag="values", bufs=STATE_BUFS)
            nc.vector.tensor_tensor(y[:], sum_1[:], y2[:], MAX)
            window = pages1[nb][:].indirect(half_list(idx4, h))
            nc.vector.tensor_tensor(window, y[:], wgo_sb[:, half_cols(h)], MULT)

        place(0, 0, fresh(0, 0))
        place(1, 0, fresh(1, 0))
        y2_of = {nb: fresh(nb, 0, "sum_a") for nb in range(2, BLOCKS - 1)}
        x1_turned = keep.tile([P, HALF // P, H], BF16, name="x1_turned", tag="turned0")
        for c in range(SLICES):
            turn_rows(x1[:, c, :], x1_turned, c, "sum_a")
        x1_grouped = turn_back(x1_turned, "grouped_a")
        h1_grouped = turn_back(h_turned[1], "grouped_c")
        place(2, 0, y2_of[2], "sum_b")
        x_q.append(quantise_half(x1_grouped, "x1", "x1_codes"))
        h_q.append(quantise_half(h1_grouped, "h1", "h1_codes"))
        behind = keep.tile([P, HALF], F32, name="behind", tag="grouped_c", align_bytes=64)
        place(3, 0, y2_of[3], "sum_b", behind)
        place(4, 0, y2_of[4])
        for nb in range(BLOCKS):
            place(nb, 1, fresh(nb, 1))
            nc.sync.dma_start(out[nb * P : (nb + 1) * P, :], pages1[nb][:])
            if nb == 0:
                place(BLOCKS - 1, 0, fresh(BLOCKS - 1, 0))
